import numpy as np
import ml_dtypes


def mxq(x, axis, fmt="e4m3"):
    dtype, down = {"e4m3": (ml_dtypes.float8_e4m3fn, 7), "e5m2": (ml_dtypes.float8_e5m2, 14)}[fmt]
    v = np.moveaxis(np.asarray(x, np.float32).astype(ml_dtypes.bfloat16).astype(np.float64), axis, -1)
    blocks = v.reshape(v.shape[:-1] + (-1, 32))
    amax = np.abs(blocks).max(-1, keepdims=True)
    byte = np.maximum(np.where(amax > 0, np.frexp(amax)[1] - 1 + 127, 0) - down, 1)
    scale = np.exp2(byte - 127.0)
    codes = (blocks / scale).astype(np.float32).astype(dtype).astype(np.float64)
    return np.moveaxis((codes * scale).reshape(v.shape), -1, axis)


WIDE = False


def mx_kscale(k):
    if not WIDE:
        return np.ones(k)
    levels = np.array([10, -10, 5, -5, 0])
    if k % 512:
        return np.exp2(np.random.permutation(np.resize(levels, k // 32))).repeat(32)
    a = np.empty((k // 512, 16))
    for p in range(k // 512):
        a[p, :8] = np.random.permutation(np.resize(levels, 8))
        for g in range(8):
            far = levels[np.abs(levels - a[p, g]) >= 10]
            a[p, g + 8] = far[np.random.randint(len(far))]
    return np.exp2(a.ravel()).repeat(32)


def f64(x):
    return np.asarray(x).astype(np.float64)


def striped(idx):
    return np.tile(idx.reshape(-1, 16).T, (8, 1)).astype(np.uint16)


def unstriped(offs):
    return offs[:16].T.reshape(-1).astype(np.int64)


E2M1 = np.array([0.0, 0.5, 1.0, 1.5, 2.0, 3.0, 4.0, 6.0, -0.0, -0.5, -1.0, -1.5, -2.0, -3.0, -4.0, -6.0])


def pack_weight(w, fmt):
    k, n = w.shape
    w = f64(np.asarray(w, np.float32).astype(ml_dtypes.bfloat16)).reshape(k // 32, 32, n)
    amax = np.abs(w).max(1)
    if fmt == "e4m3":
        byte = np.frexp(amax)[1] - 1 + 127 - 7
    else:
        mant, ex = np.frexp(amax / 6.0)
        byte = np.where(mant > 0.5, ex, ex - 1) + 127
    byte = np.clip(np.where(amax > 0, byte, 1), 1, 254)
    scaled = (w * np.exp2(127.0 - byte)[:, None, :]).reshape(k, n).astype(np.float32)
    by_word = np.ascontiguousarray(scaled.reshape(k // 512, 128, 4, n).transpose(0, 1, 3, 2))
    if fmt == "e4m3":
        words = by_word.astype(ml_dtypes.float8_e4m3fn).view(np.uint8)
    else:
        c = by_word.astype(ml_dtypes.float4_e2m1fn).view(np.uint8) & 0xF
        words = (c[..., 0::2] | (c[..., 1::2] << 4)).reshape(k // 512, 128, 2 * n)
    return np.ascontiguousarray(words), np.ascontiguousarray(byte.astype(np.uint8).reshape(k // 512, 16, n))


def unpack_weight(words, scales, fmt):
    g, _, n = scales.shape
    words = np.ascontiguousarray(words).reshape(g, 128, n, -1)
    if fmt == "e4m3":
        vals = words.view(ml_dtypes.float8_e4m3fn).astype(np.float64)
    else:
        nib = np.empty((g, 128, n, 4), np.uint8)
        nib[..., 0::2] = words & 0xF
        nib[..., 1::2] = words >> 4
        vals = E2M1[nib]
    vals = vals * np.repeat(np.exp2(scales.astype(np.float64) - 127.0), 8, axis=1)[..., None]
    return vals.transpose(0, 1, 3, 2).reshape(g * 512, n)


def silu(v):
    return v / (1.0 + np.exp(-np.maximum(v, -700.0)))


def d_silu(v):
    s = 1.0 / (1.0 + np.exp(-np.maximum(v, -700.0)))
    return s * (1.0 + v * (1.0 - s))


K, T, E, C, H, N = 256, 768, 6, 256, 512, 512


def by_expert(wq, xq):
    return np.concatenate([wq[e].T @ xq[:, e * C:(e + 1) * C] for e in range(E)], axis=1)


def setup_inputs():
    n = np.random.standard_normal
    s = mx_kscale(N)[:, None]
    u = mx_kscale(H)
    first = np.random.permutation(np.repeat(np.arange(E), T // E))
    second = (first + 1 + np.random.permutation(np.repeat(np.arange(E - 1), -(-T // (E - 1)))[:T])) % E
    while np.bincount(second, minlength=E).max() != T // E:
        load = np.bincount(second, minlength=E); hi, lo = int(load.argmax()), int(load.argmin())
        t = np.flatnonzero((second == hi) & (first != lo))[0]; second[t] = lo
    slot_token = np.empty(E * C, np.int64); pos = np.empty((2, T), np.int64); fill = np.zeros(E, np.int64)
    place = np.stack([np.random.permutation(C) for _ in range(E)])
    for r, deal in enumerate((first, second)):
        for t in np.random.permutation(T):
            e = deal[t]; j = e * C + place[e, fill[e]]; fill[e] += 1; slot_token[j] = t; pos[r, t] = j
    g = np.random.uniform(0.2, 0.8, T)
    w_slot = np.empty(E * C); w_slot[pos[0]] = g; w_slot[pos[1]] = 1.0 - g
    dy = pack_weight(n((N, T)) * s, "e4m3")
    w2 = [pack_weight(m, "e2m1") for m in n((E, N, H)) / np.sqrt(N) / s[None] * u[None, None, :]]
    w1 = [pack_weight(m, "e2m1") for m in n((E, H, K)) / np.sqrt(H) / u[None, :, None]]
    w3 = [pack_weight(m, "e2m1") for m in n((E, H, K)) / np.sqrt(H) / u[None, :, None]]
    return {
        "dy_words": dy[0],
        "dy_scales": dy[1],
        "a1": n((H, E * C)).astype(np.float32),
        "a3": n((H, E * C)).astype(np.float32),
        "w2_words": np.stack([m[0] for m in w2]),
        "w2_scales": np.stack([m[1] for m in w2]),
        "w1_words": np.stack([m[0] for m in w1]),
        "w1_scales": np.stack([m[1] for m in w1]),
        "w3_words": np.stack([m[0] for m in w3]),
        "w3_scales": np.stack([m[1] for m in w3]),
        "gate": np.tile(w_slot, (H, 1)).astype(np.float32),
        "offs": striped(slot_token),
        "pos1": striped(pos[0]),
        "pos2": striped(pos[1]),
    }


def reference(dy_words, dy_scales, a1, a3, w2_words, w2_scales, w1_words, w1_scales, w3_words, w3_scales, gate, offs, pos1, pos2):
    idx = unstriped(offs)
    w2 = np.stack([unpack_weight(w2_words[e], w2_scales[e], "e2m1") for e in range(E)])
    w1 = np.stack([unpack_weight(w1_words[e], w1_scales[e], "e2m1") for e in range(E)])
    w3 = np.stack([unpack_weight(w3_words[e], w3_scales[e], "e2m1") for e in range(E)])
    gq = unpack_weight(dy_words, dy_scales, "e4m3")[:, idx]
    dh = f64(gate) * by_expert(w2, gq)
    da1 = dh * f64(a3) * d_silu(f64(a1))
    da3 = dh * silu(f64(a1))
    dx = by_expert(w1, mxq(da1, 0, "e4m3")) + by_expert(w3, mxq(da3, 0, "e4m3"))
    return dx[:, unstriped(pos1)] + dx[:, unstriped(pos2)]

@@ -1,0 +1,240 @@
+from contextlib import ExitStack
+
+import concourse.mybir as mybir
+from concourse.masks import make_identity
+
+K, T, E, C, H, N = 256, 768, 6, 256, 512, 512
+S = E * C
+P = 128
+PACK = 4
+G = C // P
+KT = K // P
+
+FLOPS = 2 * S * (N * H + 2 * H * K)
+BYTES = 4 * (2 * H * S + S + K * T) + (N * T + N * T // 32) + E * (N * H + 2 * H * K) * 17 // 32 + 2 * P * (S + 2 * T) // 16
+
+F32 = mybir.dt.float32
+BF16 = mybir.dt.bfloat16
+I32 = mybir.dt.int32
+U32 = mybir.dt.uint32
+U16 = mybir.dt.uint16
+U8 = mybir.dt.uint8
+FP8X4 = mybir.dt.float8_e4m3fn_x4
+FP4X4 = mybir.dt.float4_e2m1fn_x4
+ACT = mybir.ActivationFunctionType
+ALU = mybir.AluOpType
+
+
+def tile_moe_bdx_glu_silu_kernel(
+    tc, dy_words, dy_scales, a1, a3, w2_words, w2_scales, w1_words, w1_scales,
+    w3_words, w3_scales, gate, offs, pos1, pos2, out,
+):
+    nc = tc.nc
+    with ExitStack() as ctx:
+        keep = ctx.enter_context(tc.tile_pool(name="keep", bufs=1))
+        ring = ctx.enter_context(tc.tile_pool(name="ring", bufs=3))
+        psum_dh = ctx.enter_context(tc.psum_pool(name="psum_dh", bufs=2))
+        psum_turn = ctx.enter_context(tc.psum_pool(name="psum_turn", bufs=3))
+        psum_dx = ctx.enter_context(tc.psum_pool(name="psum_dx", bufs=2))
+        psum_gate = ctx.enter_context(tc.psum_pool(name="psum_gate", bufs=1))
+
+        offs_sb = keep.tile([P, S // 16], U16, name="offs_sb")
+        pos1_sb = keep.tile([P, T // 16], U16, name="pos1_sb")
+        pos2_sb = keep.tile([P, T // 16], U16, name="pos2_sb")
+        dy_w = keep.tile([P, T], I32, name="dy_w", align_bytes=64)
+        dy_s = keep.tile([P, T], U8, name="dy_s", align_bytes=64)
+        g_w = keep.tile([P, S], U32, name="g_w", align_bytes=64)
+        g_s = keep.tile([P, S], U8, name="g_s", align_bytes=64)
+        w2_w = keep.tile([P, E, 2 * H], U8, name="w2_w", align_bytes=64)
+        w1_w = keep.tile([P, E, 2 * K], U8, name="w1_w", align_bytes=64)
+        w3_w = keep.tile([P, E, 2 * K], U8, name="w3_w", align_bytes=64)
+        w2_s = keep.tile([P, E, H], U8, name="w2_s", align_bytes=64)
+        w1_s = keep.tile([P, E, K], U8, name="w1_s", align_bytes=64)
+        w3_s = keep.tile([P, E, K], U8, name="w3_s", align_bytes=64)
+        gate_rows = keep.tile([P, P], F32, name="gate_rows")
+        gate_col = keep.tile([P, E * G], F32, name="gate_col")
+        ident = keep.tile([P, P], F32, name="ident")
+        a1_sb = [keep.tile([P, PACK, C], F32, name="a1_%d" % e) for e in range(E)]
+        a3_sb = [keep.tile([P, PACK, C], F32, name="a3_%d" % e) for e in range(E)]
+        s_sb = [keep.tile([P, PACK, C], F32, name="s_%d" % e) for e in range(E)]
+        q_sb = [keep.tile([P, PACK, C], F32, name="q_%d" % e) for e in range(E)]
+        dx = [keep.tile([P, S], F32, name="dx_%d" % kt) for kt in range(KT)]
+
+        for plane in (dy_s, w2_s, w1_s, w3_s):
+            nc.vector.memset(plane[:].bitcast(I32), 0)
+        make_identity(nc, ident[:])
+
+        def load_scales(plane, src):
+            for quad in range(4):
+                nc.sync.dma_start(
+                    out=plane[32 * quad : 32 * quad + 4, :, :].bitcast(I32),
+                    in_=src[:, 0, 4 * quad : 4 * quad + 4, :].rearrange("e r i -> r e i").bitcast(I32),
+                )
+
+        def load_words(tile, src, e0, e1):
+            nc.sync.dma_start(
+                out=tile[:, e0:e1, :].bitcast(I32),
+                in_=src[e0:e1, 0, :, :].rearrange("e p b -> p e b").bitcast(I32),
+            )
+
+        def load_saved(tile, src, e):
+            nc.sync.dma_start(
+                out=tile[:], in_=src[:, e * C : (e + 1) * C].rearrange("(p t) c -> p t c", t=PACK)
+            )
+
+        nc.sync.dma_start(offs_sb[:], offs)
+        nc.sync.dma_start(out=dy_w[:], in_=dy_words[0].rearrange("p t d -> p (t d)").bitcast(I32))
+        for quad in range(4):
+            nc.sync.dma_start(
+                out=dy_s[32 * quad : 32 * quad + 4, :].bitcast(I32),
+                in_=dy_scales[0, 4 * quad : 4 * quad + 4, :].bitcast(I32),
+            )
+        load_saved(a1_sb[0], a1, 0)
+        nc.sync.dma_start(out=gate_rows[:], in_=gate.rearrange("h (g p) -> (h g) p", p=P)[0:P, :])
+        load_scales(w2_s, w2_scales)
+        load_words(w2_w, w2_words, 0, 2)
+        load_saved(a3_sb[0], a3, 0)
+        load_saved(a1_sb[1], a1, 1)
+        load_saved(a3_sb[1], a3, 1)
+        load_scales(w1_s, w1_scales)
+        load_scales(w3_s, w3_scales)
+        load_saved(a1_sb[2], a1, 2)
+        load_words(w1_w, w1_words, 0, E)
+        load_words(w3_w, w3_words, 0, E)
+        load_words(w2_w, w2_words, 2, E)
+        load_saved(a3_sb[2], a3, 2)
+        for e in range(3, E):
+            load_saved(a1_sb[e], a1, e)
+            load_saved(a3_sb[e], a3, e)
+        nc.sync.dma_start(pos1_sb[:], pos1)
+        nc.sync.dma_start(pos2_sb[:], pos2)
+
+        gate_ps = psum_gate.tile([P, P], F32, name="gate_ps")
+        nc.tensor.transpose(gate_ps[:], gate_rows[:], ident[:])
+        nc.scalar.copy(gate_col[:], gate_ps[:, 0 : E * G])
+
+        def gather_words(j0, j1):
+            nc.vector.tensor_copy(g_w[:, j0:j1], dy_w[:].bitcast(U32).indirect(offs_sb[:, j0 // 16 : j1 // 16]))
+
+        def gather_bytes(j0, j1):
+            nc.vector.tensor_copy(g_s[:, j0:j1], dy_s[:].indirect(offs_sb[:, j0 // 16 : j1 // 16]))
+
+        def activations(e):
+            th = ring.tile([P, PACK, C], F32, name="th")
+            nc.scalar.activation(s_sb[e][:], a1_sb[e][:], ACT.Silu)
+            nc.scalar.activation(th[:], a1_sb[e][:], ACT.Tanh, scale=0.5)
+            nc.scalar.activation(q_sb[e][:], th[:], ACT.Identity, bias=0.5, scale=-0.5)
+
+        dh = {}
+
+        def first_product(e, g):
+            cols = slice(e * C + g * P, e * C + (g + 1) * P)
+            acc = psum_dh.tile([P, H], F32, name="acc")
+            nc.tensor.matmul_mx(
+                out=acc[:], lhsT=g_w[:, cols].bitcast(FP8X4), lhsT_scale=g_s[:, cols],
+                rhs=w2_w[:, e, :].bitcast(FP4X4), rhs_scale=w2_s[:, e, :], start=True, stop=True,
+            )
+            gated = ring.tile([P, PACK, P], F32, name="gated")
+            nc.scalar.activation(
+                gated[:], acc[:].rearrange("j (p t) -> j t p", t=PACK), ACT.Copy,
+                scale=gate_col[:, e * G + g : e * G + g + 1],
+            )
+            turned = psum_turn.tile([P, PACK, P], F32, name="turned")
+            for t in range(PACK):
+                nc.tensor.transpose(turned[:, t, :], gated[:, t, :], ident[:])
+            dh[e, g] = turned
+
+        x_sb, u_sb, da_sb, codes, scales = {}, {}, {}, {}, {}
+
+        def make_x(e):
+            x_sb[e] = ring.tile([P, PACK, C], F32, name="x")
+            nc.vector.scalar_tensor_tensor(x_sb[e][:], s_sb[e][:], -1.0, q_sb[e][:], ALU.add, ALU.mult)
+
+        def make_u(e):
+            u_sb[e] = ring.tile([P, PACK, C], F32, name="u")
+            nc.vector.scalar_tensor_tensor(u_sb[e][:], x_sb[e][:], 1.0, a3_sb[e][:], ALU.add, ALU.mult)
+
+        def make_da(e, g, w):
+            if (g, w) == (0, 1):
+                da_sb[e] = ring.tile([P, G, 2, P * PACK], BF16, name="da", align_bytes=64)
+                codes[e] = ring.tile([P, G, 2, P], U32, name="codes", align_bytes=64)
+                scales[e] = ring.tile([P, G, 2, P], U8, name="scales", align_bytes=64)
+            factor = (u_sb[e], s_sb[e])[w]
+            nc.vector.tensor_tensor(
+                da_sb[e][:, g, w, :].rearrange("p (c i t) -> p c t i", i=4, t=PACK),
+                dh[e, g][:].rearrange("p t (c i) -> p c t i", i=4),
+                factor[:, :, g * P : (g + 1) * P].rearrange("p t (c i) -> p c t i", i=4),
+                ALU.mult,
+            )
+
+        def quantize(e, g0, g1):
+            nc.vector.quantize_mx(
+                out=codes[e][:, g0:g1, :, :].rearrange("p g w j -> p (g w j)").bitcast(FP8X4),
+                scales=scales[e][:, g0:g1, :, :].rearrange("p g w j -> p (g w j)"),
+                in_=da_sb[e][:, g0:g1, :, :].rearrange("p g w j -> p (g w j)"),
+            )
+
+        def second_product(e, g0, g1):
+            for kt in range(KT):
+                acc = psum_dx.tile([P, (g1 - g0) * P], F32, name="acc_dx")
+                for g in range(g0, g1):
+                    for w, (words, plane) in enumerate(((w1_w, w1_s), (w3_w, w3_s))):
+                        nc.tensor.matmul_mx(
+                            out=acc[:, (g - g0) * P : (g - g0 + 1) * P],
+                            lhsT=words[:, e, 2 * kt * P : 2 * (kt + 1) * P].bitcast(FP4X4),
+                            lhsT_scale=plane[:, e, kt * P : (kt + 1) * P],
+                            rhs=codes[e][:, g, w, :].bitcast(FP8X4),
+                            rhs_scale=scales[e][:, g, w, :],
+                            start=(w == 0), stop=(w == 1),
+                        )
+                nc.scalar.copy(dx[kt][:, e * C + g0 * P : e * C + g1 * P], acc[:])
+
+        gather_words(0, 2 * C)
+        gather_bytes(0, 2 * C)
+        activations(0)
+        first_product(0, 0)
+        first_product(0, 1)
+        activations(1)
+        gather_words(2 * C, 4 * C)
+        gather_bytes(2 * C, 4 * C)
+        make_x(0)
+        gather_words(4 * C, 6 * C)
+        make_u(0)
+        gather_bytes(4 * C, 6 * C)
+        for e in range(E):
+            last = e == E - 1
+            make_da(e, 0, 1)
+            make_da(e, 0, 0)
+            if not last:
+                first_product(e + 1, 0)
+                make_x(e + 1)
+            make_da(e, 1, 1)
+            if last:
+                quantize(e, 0, 1)
+                second_product(e, 0, 1)
+            make_da(e, 1, 0)
+            if not last:
+                first_product(e + 1, 1)
+                make_u(e + 1)
+                quantize(e, 0, G)
+                second_product(e, 0, G)
+                if e + 2 < E:
+                    activations(e + 2)
+            else:
+                quantize(e, 1, G)
+                second_product(e, 1, G)
+
+        half = T // 2
+        for kt in range(KT):
+            first = keep.tile([P, T], F32, name="first_%d" % kt)
+            second = keep.tile([P, T], F32, name="second_%d" % kt)
+            total = keep.tile([P, T], F32, name="total_%d" % kt)
+            nc.vector.tensor_copy(first[:], dx[kt][:].indirect(pos1_sb[:]))
+            for t0 in (0, half):
+                nc.vector.tensor_copy(
+                    second[:, t0 : t0 + half], dx[kt][:].indirect(pos2_sb[:, t0 // 16 : (t0 + half) // 16])
+                )
+            for t0 in (0, half):
+                cols = slice(t0, t0 + half)
+                nc.vector.tensor_tensor(total[:, cols], first[:, cols], second[:, cols], ALU.add)
+                nc.sync.dma_start(out=out[kt * P : (kt + 1) * P, cols], in_=total[:, cols])

@@ -33,10 +33,11 @@ def tile_moe_bdx_glu_silu_kernel(
     with ExitStack() as ctx:
         keep = ctx.enter_context(tc.tile_pool(name="keep", bufs=1))
         ring = ctx.enter_context(tc.tile_pool(name="ring", bufs=3))
+        shared = ctx.enter_context(tc.tile_pool(name="shared", bufs=1))
+        psum_a1 = ctx.enter_context(tc.psum_pool(name="psum_a1", bufs=2))
         psum_dh = ctx.enter_context(tc.psum_pool(name="psum_dh", bufs=2))
-        psum_turn = ctx.enter_context(tc.psum_pool(name="psum_turn", bufs=3))
+        psum_turn = ctx.enter_context(tc.psum_pool(name="psum_turn", bufs=2))
         psum_dx = ctx.enter_context(tc.psum_pool(name="psum_dx", bufs=2))
-        psum_gate = ctx.enter_context(tc.psum_pool(name="psum_gate", bufs=1))
 
         offs_sb = keep.tile([P, S // 16], U16, name="offs_sb")
         pos1_sb = keep.tile([P, T // 16], U16, name="pos1_sb")
@@ -56,8 +57,6 @@ def tile_moe_bdx_glu_silu_kernel(
         ident = keep.tile([P, P], F32, name="ident")
         a1_sb = [keep.tile([P, PACK, C], F32, name="a1_%d" % e) for e in range(E)]
         a3_sb = [keep.tile([P, PACK, C], F32, name="a3_%d" % e) for e in range(E)]
-        s_sb = [keep.tile([P, PACK, C], F32, name="s_%d" % e) for e in range(E)]
-        q_sb = [keep.tile([P, PACK, C], F32, name="q_%d" % e) for e in range(E)]
         dx = [keep.tile([P, S], F32, name="dx_%d" % kt) for kt in range(KT)]
 
         for plane in (dy_s, w2_s, w1_s, w3_s):
@@ -82,34 +81,40 @@ def tile_moe_bdx_glu_silu_kernel(
                 out=tile[:], in_=src[:, e * C : (e + 1) * C].rearrange("(p t) c -> p t c", t=PACK)
             )
 
-        nc.sync.dma_start(offs_sb[:], offs)
         nc.sync.dma_start(out=dy_w[:], in_=dy_words[0].rearrange("p t d -> p (t d)").bitcast(I32))
+        nc.sync.dma_start(offs_sb[:], offs)
+        load_saved(a1_sb[0], a1, 0)
         for quad in range(4):
             nc.sync.dma_start(
                 out=dy_s[32 * quad : 32 * quad + 4, :].bitcast(I32),
                 in_=dy_scales[0, 4 * quad : 4 * quad + 4, :].bitcast(I32),
             )
-        load_saved(a1_sb[0], a1, 0)
+        load_saved(a3_sb[0], a3, 0)
+        load_saved(a1_sb[1], a1, 1)
         nc.sync.dma_start(out=gate_rows[:], in_=gate.rearrange("h (g p) -> (h g) p", p=P)[0:P, :])
         load_scales(w2_s, w2_scales)
         load_words(w2_w, w2_words, 0, 2)
-        load_saved(a3_sb[0], a3, 0)
-        load_saved(a1_sb[1], a1, 1)
         load_saved(a3_sb[1], a3, 1)
+        load_saved(a1_sb[2], a1, 2)
         load_scales(w1_s, w1_scales)
         load_scales(w3_s, w3_scales)
-        load_saved(a1_sb[2], a1, 2)
-        load_words(w1_w, w1_words, 0, E)
-        load_words(w3_w, w3_words, 0, E)
-        load_words(w2_w, w2_words, 2, E)
+        load_words(w1_w, w1_words, 0, 2)
+        load_words(w3_w, w3_words, 0, 2)
+        load_saved(a1_sb[3], a1, 3)
         load_saved(a3_sb[2], a3, 2)
-        for e in range(3, E):
-            load_saved(a1_sb[e], a1, e)
-            load_saved(a3_sb[e], a3, e)
+        load_words(w2_w, w2_words, 2, 4)
+        load_saved(a1_sb[4], a1, 4)
+        load_saved(a3_sb[3], a3, 3)
+        load_words(w1_w, w1_words, 2, E)
+        load_words(w3_w, w3_words, 2, E)
+        load_saved(a1_sb[5], a1, 5)
+        load_saved(a3_sb[4], a3, 4)
+        load_words(w2_w, w2_words, 4, E)
+        load_saved(a3_sb[5], a3, 5)
         nc.sync.dma_start(pos1_sb[:], pos1)
         nc.sync.dma_start(pos2_sb[:], pos2)
 
-        gate_ps = psum_gate.tile([P, P], F32, name="gate_ps")
+        gate_ps = psum_dx.tile([P, P], F32, name="gate_ps", tag="acc_dx")
         nc.tensor.transpose(gate_ps[:], gate_rows[:], ident[:])
         nc.scalar.copy(gate_col[:], gate_ps[:, 0 : E * G])
 
@@ -119,50 +124,60 @@ def tile_moe_bdx_glu_silu_kernel(
         def gather_bytes(j0, j1):
             nc.vector.tensor_copy(g_s[:, j0:j1], dy_s[:].indirect(offs_sb[:, j0 // 16 : j1 // 16]))
 
-        def activations(e):
-            th = ring.tile([P, PACK, C], F32, name="th")
-            nc.scalar.activation(s_sb[e][:], a1_sb[e][:], ACT.Silu)
-            nc.scalar.activation(th[:], a1_sb[e][:], ACT.Tanh, scale=0.5)
-            nc.scalar.activation(q_sb[e][:], th[:], ACT.Identity, bias=0.5, scale=-0.5)
+        one_less, y_sb, sig, turned, da_sb, codes, scales = {}, {}, {}, {}, {}, {}, {}
+        slot_bytes = 4 * PACK * C
 
-        dh = {}
+        def make_one_less(e):
+            neg = ring.tile([P, PACK, C], F32, name="neg")
+            one_less[e] = ring.tile([P, PACK, C], F32, name="one_less")
+            nc.scalar.activation(neg[:], a1_sb[e][:], ACT.Silu, scale=-1.0)
+            if e < 4:
+                nc.gpsimd.tensor_scalar(one_less[e][:], neg[:], -1.0, 1.0, ALU.mult, ALU.add)
+            else:
+                nc.scalar.activation(one_less[e][:], neg[:], ACT.Identity, bias=1.0, scale=-1.0)
 
-        def first_product(e, g):
-            cols = slice(e * C + g * P, e * C + (g + 1) * P)
+        def make_y(e):
+            y_sb[e] = shared.tile([P, PACK, C], F32, name="y_%d" % e, offset=slot_bytes * (e % 3), align_bytes=64)
+            nc.gpsimd.tensor_tensor(y_sb[e][:], one_less[e][:], a3_sb[e][:], ALU.mult)
+
+        def make_sigmoid(n):
+            e, g = divmod(n, G)
+            a1_t = psum_a1.tile([P, PACK, P], F32, name="a1_t")
+            for t in range(PACK):
+                nc.tensor.transpose(a1_t[:, t, :], a1_sb[e][:, t, g * P : (g + 1) * P], ident[:])
+            th = ring.tile([P, PACK, P], F32, name="th")
+            sig[n] = ring.tile([P, PACK, P], F32, name="sig", bufs=6)
+            nc.scalar.activation(th[:], a1_t[:], ACT.Tanh, scale=0.5)
+            nc.scalar.activation(sig[n][:], th[:], ACT.Identity, bias=0.5, scale=0.5)
+
+        def first_product(n):
+            e = n // G
+            cols = slice(n * P, (n + 1) * P)
             acc = psum_dh.tile([P, H], F32, name="acc")
             nc.tensor.matmul_mx(
                 out=acc[:], lhsT=g_w[:, cols].bitcast(FP8X4), lhsT_scale=g_s[:, cols],
                 rhs=w2_w[:, e, :].bitcast(FP4X4), rhs_scale=w2_s[:, e, :], start=True, stop=True,
             )
-            gated = ring.tile([P, PACK, P], F32, name="gated")
-            nc.scalar.activation(
-                gated[:], acc[:].rearrange("j (p t) -> j t p", t=PACK), ACT.Copy,
-                scale=gate_col[:, e * G + g : e * G + g + 1],
+            m = ring.tile([P, PACK, P], F32, name="m")
+            nc.vector.scalar_tensor_tensor(
+                m[:], acc[:].rearrange("j (p t) -> j t p", t=PACK), gate_col[:, n : n + 1], sig[n][:],
+                ALU.mult, ALU.mult,
             )
-            turned = psum_turn.tile([P, PACK, P], F32, name="turned")
+            turned[n] = psum_turn.tile([P, PACK, P], F32, name="turned")
             for t in range(PACK):
-                nc.tensor.transpose(turned[:, t, :], gated[:, t, :], ident[:])
-            dh[e, g] = turned
-
-        x_sb, u_sb, da_sb, codes, scales = {}, {}, {}, {}, {}
-
-        def make_x(e):
-            x_sb[e] = ring.tile([P, PACK, C], F32, name="x")
-            nc.vector.scalar_tensor_tensor(x_sb[e][:], s_sb[e][:], -1.0, q_sb[e][:], ALU.add, ALU.mult)
-
-        def make_u(e):
-            u_sb[e] = ring.tile([P, PACK, C], F32, name="u")
-            nc.vector.scalar_tensor_tensor(u_sb[e][:], x_sb[e][:], 1.0, a3_sb[e][:], ALU.add, ALU.mult)
+                nc.tensor.transpose(turned[n][:, t, :], m[:, t, :], ident[:])
 
         def make_da(e, g, w):
             if (g, w) == (0, 1):
-                da_sb[e] = ring.tile([P, G, 2, P * PACK], BF16, name="da", align_bytes=64)
+                da_sb[e] = shared.tile(
+                    [P, G, 2, P * PACK], BF16, name="da_%d" % e, offset=slot_bytes * ((e + 2) % 3), align_bytes=64
+                )
                 codes[e] = ring.tile([P, G, 2, P], U32, name="codes", align_bytes=64)
                 scales[e] = ring.tile([P, G, 2, P], U8, name="scales", align_bytes=64)
-            factor = (u_sb[e], s_sb[e])[w]
+            factor = (y_sb[e], a1_sb[e])[w]
             nc.vector.tensor_tensor(
                 da_sb[e][:, g, w, :].rearrange("p (c i t) -> p c t i", i=4, t=PACK),
-                dh[e, g][:].rearrange("p t (c i) -> p c t i", i=4),
+                turned[e * G + g][:].rearrange("p t (c i) -> p c t i", i=4),
                 factor[:, :, g * P : (g + 1) * P].rearrange("p t (c i) -> p c t i", i=4),
                 ALU.mult,
             )
@@ -189,52 +204,53 @@ def tile_moe_bdx_glu_silu_kernel(
                         )
                 nc.scalar.copy(dx[kt][:, e * C + g0 * P : e * C + g1 * P], acc[:])
 
-        gather_words(0, 2 * C)
-        gather_bytes(0, 2 * C)
-        activations(0)
-        first_product(0, 0)
-        first_product(0, 1)
-        activations(1)
-        gather_words(2 * C, 4 * C)
-        gather_bytes(2 * C, 4 * C)
-        make_x(0)
-        gather_words(4 * C, 6 * C)
-        make_u(0)
-        gather_bytes(4 * C, 6 * C)
+        for j in range(0, S, 2 * C):
+            gather_words(j, j + 2 * C)
+            gather_bytes(j, j + 2 * C)
+        make_one_less(0)
+        make_y(0)
+        make_sigmoid(0)
+        make_sigmoid(1)
+        make_one_less(1)
+        make_y(1)
+        first_product(0)
+        make_sigmoid(2)
         for e in range(E):
             last = e == E - 1
+            n = e * G
+            first_product(n + 1)
+            if e > 0:
+                quantize(e - 1, 0, G)
+                if e + 1 < E:
+                    make_y(e + 1)
+                second_product(e - 1, 0, G)
+            if n + 3 < E * G:
+                make_sigmoid(n + 3)
+            if e + 2 < E:
+                make_one_less(e + 2)
             make_da(e, 0, 1)
             make_da(e, 0, 0)
             if not last:
-                first_product(e + 1, 0)
-                make_x(e + 1)
+                first_product(n + 2)
+            if n + 4 < E * G:
+                make_sigmoid(n + 4)
             make_da(e, 1, 1)
             if last:
                 quantize(e, 0, 1)
                 second_product(e, 0, 1)
             make_da(e, 1, 0)
-            if not last:
-                first_product(e + 1, 1)
-                make_u(e + 1)
-                quantize(e, 0, G)
-                second_product(e, 0, G)
-                if e + 2 < E:
-                    activations(e + 2)
-            else:
-                quantize(e, 1, G)
-                second_product(e, 1, G)
+        quantize(E - 1, 1, G)
+        second_product(E - 1, 1, G)
 
-        half = T // 2
         for kt in range(KT):
             first = keep.tile([P, T], F32, name="first_%d" % kt)
             second = keep.tile([P, T], F32, name="second_%d" % kt)
             total = keep.tile([P, T], F32, name="total_%d" % kt)
-            nc.vector.tensor_copy(first[:], dx[kt][:].indirect(pos1_sb[:]))
-            for t0 in (0, half):
-                nc.vector.tensor_copy(
-                    second[:, t0 : t0 + half], dx[kt][:].indirect(pos2_sb[:, t0 // 16 : (t0 + half) // 16])
-                )
-            for t0 in (0, half):
-                cols = slice(t0, t0 + half)
-                nc.vector.tensor_tensor(total[:, cols], first[:, cols], second[:, cols], ALU.add)
+            pieces = ((0, T),) if kt < KT - 1 else ((0, 512), (512, T))
+            for t0, t1 in pieces:
+                cols = slice(t0, t1)
+                nc.vector.tensor_copy(first[:, cols], dx[kt][:].indirect(pos1_sb[:, t0 // 16 : t1 // 16]))
+                nc.vector.tensor_copy(second[:, cols], dx[kt][:].indirect(pos2_sb[:, t0 // 16 : t1 // 16]))
+                adder = nc.vector if (kt, t1) == (KT - 1, T) else nc.gpsimd
+                adder.tensor_tensor(total[:, cols], first[:, cols], second[:, cols], ALU.add)
                 nc.sync.dma_start(out=out[kt * P : (kt + 1) * P, cols], in_=total[:, cols])

@@ -33,19 +33,18 @@ def tile_moe_bdx_glu_silu_kernel(
     with ExitStack() as ctx:
         keep = ctx.enter_context(tc.tile_pool(name="keep", bufs=1))
         ring = ctx.enter_context(tc.tile_pool(name="ring", bufs=3))
-        shared = ctx.enter_context(tc.tile_pool(name="shared", bufs=1))
         psum_a1 = ctx.enter_context(tc.psum_pool(name="psum_a1", bufs=2))
         psum_dh = ctx.enter_context(tc.psum_pool(name="psum_dh", bufs=2))
-        psum_turn = ctx.enter_context(tc.psum_pool(name="psum_turn", bufs=2))
-        psum_dx = ctx.enter_context(tc.psum_pool(name="psum_dx", bufs=2))
+        psum_turn = ctx.enter_context(tc.psum_pool(name="psum_turn", bufs=3))
+        psum_dx = ctx.enter_context(tc.psum_pool(name="psum_dx", bufs=1))
 
         offs_sb = keep.tile([P, S // 16], U16, name="offs_sb")
         pos1_sb = keep.tile([P, T // 16], U16, name="pos1_sb")
         pos2_sb = keep.tile([P, T // 16], U16, name="pos2_sb")
         dy_w = keep.tile([P, T], I32, name="dy_w", align_bytes=64)
         dy_s = keep.tile([P, T], U8, name="dy_s", align_bytes=64)
-        g_w = keep.tile([P, S], U32, name="g_w", align_bytes=64)
-        g_s = keep.tile([P, S], U8, name="g_s", align_bytes=64)
+        g_w = keep.tile([P, S - C], U32, name="g_w", align_bytes=64)
+        g_s = keep.tile([P, S - C], U8, name="g_s", align_bytes=64)
         w2_w = keep.tile([P, E, 2 * H], U8, name="w2_w", align_bytes=64)
         w1_w = keep.tile([P, E, 2 * K], U8, name="w1_w", align_bytes=64)
         w3_w = keep.tile([P, E, 2 * K], U8, name="w3_w", align_bytes=64)
@@ -57,15 +56,17 @@ def tile_moe_bdx_glu_silu_kernel(
         ident = keep.tile([P, P], F32, name="ident")
         a1_sb = [keep.tile([P, PACK, C], F32, name="a1_%d" % e) for e in range(E)]
         a3_sb = [keep.tile([P, PACK, C], F32, name="a3_%d" % e) for e in range(E)]
-        dx = [keep.tile([P, S], F32, name="dx_%d" % kt) for kt in range(KT)]
+        dx = keep.tile([P, KT, S], F32, name="dx")
 
-        for plane in (dy_s, w2_s, w1_s, w3_s):
-            nc.vector.memset(plane[:].bitcast(I32), 0)
         make_identity(nc, ident[:])
+        nc.vector.memset(dy_s[:].bitcast(I32), 0)
+        nc.vector.memset(w2_s[:].bitcast(I32), 0)
+        nc.vector.memset(w1_s[:].bitcast(I32), 0)
+        nc.vector.memset(w3_s[:].bitcast(I32), 0)
 
-        def load_scales(plane, src):
-            for quad in range(4):
-                nc.sync.dma_start(
+        def load_scales(queue, plane, src, quads):
+            for quad in quads:
+                queue.dma_start(
                     out=plane[32 * quad : 32 * quad + 4, :, :].bitcast(I32),
                     in_=src[:, 0, 4 * quad : 4 * quad + 4, :].rearrange("e r i -> r e i").bitcast(I32),
                 )
@@ -83,33 +84,30 @@ def tile_moe_bdx_glu_silu_kernel(
 
         nc.sync.dma_start(out=dy_w[:], in_=dy_words[0].rearrange("p t d -> p (t d)").bitcast(I32))
         nc.sync.dma_start(offs_sb[:], offs)
-        load_saved(a1_sb[0], a1, 0)
         for quad in range(4):
             nc.sync.dma_start(
                 out=dy_s[32 * quad : 32 * quad + 4, :].bitcast(I32),
                 in_=dy_scales[0, 4 * quad : 4 * quad + 4, :].bitcast(I32),
             )
-        load_saved(a3_sb[0], a3, 0)
-        load_saved(a1_sb[1], a1, 1)
         nc.sync.dma_start(out=gate_rows[:], in_=gate.rearrange("h (g p) -> (h g) p", p=P)[0:P, :])
-        load_scales(w2_s, w2_scales)
+        load_saved(a1_sb[0], a1, 0)
+        load_scales(nc.sync, w2_s, w2_scales, range(4))
+        load_saved(a1_sb[1], a1, 1)
         load_words(w2_w, w2_words, 0, 2)
-        load_saved(a3_sb[1], a3, 1)
+        load_saved(a3_sb[0], a3, 0)
         load_saved(a1_sb[2], a1, 2)
-        load_scales(w1_s, w1_scales)
-        load_scales(w3_s, w3_scales)
-        load_words(w1_w, w1_words, 0, 2)
-        load_words(w3_w, w3_words, 0, 2)
+        load_words(w2_w, w2_words, 2, 6)
+        load_saved(a3_sb[1], a3, 1)
         load_saved(a1_sb[3], a1, 3)
         load_saved(a3_sb[2], a3, 2)
-        load_words(w2_w, w2_words, 2, 4)
         load_saved(a1_sb[4], a1, 4)
+        load_scales(nc.sync, w1_s, w1_scales, range(4))
         load_saved(a3_sb[3], a3, 3)
-        load_words(w1_w, w1_words, 2, E)
-        load_words(w3_w, w3_words, 2, E)
         load_saved(a1_sb[5], a1, 5)
+        load_scales(nc.sync, w3_s, w3_scales, range(4))
+        load_words(w1_w, w1_words, 0, 6)
+        load_words(w3_w, w3_words, 0, 6)
         load_saved(a3_sb[4], a3, 4)
-        load_words(w2_w, w2_words, 4, E)
         load_saved(a3_sb[5], a3, 5)
         nc.sync.dma_start(pos1_sb[:], pos1)
         nc.sync.dma_start(pos2_sb[:], pos2)
@@ -119,48 +117,52 @@ def tile_moe_bdx_glu_silu_kernel(
         nc.scalar.copy(gate_col[:], gate_ps[:, 0 : E * G])
 
         def gather_words(j0, j1):
-            nc.vector.tensor_copy(g_w[:, j0:j1], dy_w[:].bitcast(U32).indirect(offs_sb[:, j0 // 16 : j1 // 16]))
+            nc.vector.tensor_copy(g_w[:, j0 % (S - C) : j0 % (S - C) + j1 - j0], dy_w[:].bitcast(U32).indirect(offs_sb[:, j0 // 16 : j1 // 16]))
 
         def gather_bytes(j0, j1):
-            nc.vector.tensor_copy(g_s[:, j0:j1], dy_s[:].indirect(offs_sb[:, j0 // 16 : j1 // 16]))
+            nc.vector.tensor_copy(g_s[:, j0 % (S - C) : j0 % (S - C) + j1 - j0], dy_s[:].indirect(offs_sb[:, j0 // 16 : j1 // 16]))
 
-        one_less, y_sb, sig, turned, da_sb, codes, scales = {}, {}, {}, {}, {}, {}, {}
-        slot_bytes = 4 * PACK * C
+        neg, y_sb, turned, da_sb, codes, scales = {}, {}, {}, {}, {}, {}
+        sig = keep.tile([P, E * G, PACK, P], F32, name="sig")
 
-        def make_one_less(e):
-            neg = ring.tile([P, PACK, C], F32, name="neg")
-            one_less[e] = ring.tile([P, PACK, C], F32, name="one_less")
-            nc.scalar.activation(neg[:], a1_sb[e][:], ACT.Silu, scale=-1.0)
-            if e < 4:
-                nc.gpsimd.tensor_scalar(one_less[e][:], neg[:], -1.0, 1.0, ALU.mult, ALU.add)
-            else:
-                nc.scalar.activation(one_less[e][:], neg[:], ACT.Identity, bias=1.0, scale=-1.0)
+        def make_neg(e):
+            neg[e] = ring.tile([P, PACK, C], F32, name="neg")
+            nc.scalar.activation(neg[e][:], a1_sb[e][:], ACT.Silu, scale=-1.0)
 
         def make_y(e):
-            y_sb[e] = shared.tile([P, PACK, C], F32, name="y_%d" % e, offset=slot_bytes * (e % 3), align_bytes=64)
-            nc.gpsimd.tensor_tensor(y_sb[e][:], one_less[e][:], a3_sb[e][:], ALU.mult)
+            if e < 2:
+                y_sb[e] = keep.tile([P, G, PACK, P], F32, name="y_%d" % e)[:]
+            else:
+                y_sb[e] = sig[:, e * G - 1 : e * G + 1, :, :]
+            by_row = y_sb[e].rearrange("p g t j -> p t g j")
+            nc.gpsimd.tensor_scalar(by_row, neg[e][:].rearrange("p t (g j) -> p t g j", g=G), -1.0, 1.0, ALU.mult, ALU.add)
+            nc.gpsimd.tensor_tensor(by_row, by_row, a3_sb[e][:].rearrange("p t (g j) -> p t g j", g=G), ALU.mult)
 
-        def make_sigmoid(n):
-            e, g = divmod(n, G)
-            a1_t = psum_a1.tile([P, PACK, P], F32, name="a1_t")
-            for t in range(PACK):
-                nc.tensor.transpose(a1_t[:, t, :], a1_sb[e][:, t, g * P : (g + 1) * P], ident[:])
-            th = ring.tile([P, PACK, P], F32, name="th")
-            sig[n] = ring.tile([P, PACK, P], F32, name="sig", bufs=6)
-            nc.scalar.activation(th[:], a1_t[:], ACT.Tanh, scale=0.5)
-            nc.scalar.activation(sig[n][:], th[:], ACT.Identity, bias=0.5, scale=0.5)
+        def make_sigmoid(e):
+            th = []
+            for g in range(G):
+                a1_t = psum_a1.tile([P, PACK, P], F32, name="a1_t")
+                for t in range(PACK):
+                    nc.tensor.transpose(a1_t[:, t, :], a1_sb[e][:, t, g * P : (g + 1) * P], ident[:])
+                th.append(ring.tile([P, PACK, P], F32, name="th"))
+                nc.scalar.activation(th[g][:], a1_t[:], ACT.Tanh, scale=0.5)
+            for g in range(G):
+                nc.scalar.activation(sig[:, e * G + g, :, :], th[g][:], ACT.Identity, bias=0.5, scale=0.5)
 
         def first_product(n):
             e = n // G
-            cols = slice(n * P, (n + 1) * P)
+            cols = slice(n * P % (S - C), n * P % (S - C) + P)
             acc = psum_dh.tile([P, H], F32, name="acc")
             nc.tensor.matmul_mx(
                 out=acc[:], lhsT=g_w[:, cols].bitcast(FP8X4), lhsT_scale=g_s[:, cols],
                 rhs=w2_w[:, e, :].bitcast(FP4X4), rhs_scale=w2_s[:, e, :], start=True, stop=True,
             )
-            m = ring.tile([P, PACK, P], F32, name="m")
+            if n < 3:
+                m = ring.tile([P, PACK, P], F32, name="m")[:]
+            else:
+                m = y_sb[(n - 3) // G][:, (n - 3) % G, :, :]
             nc.vector.scalar_tensor_tensor(
-                m[:], acc[:].rearrange("j (p t) -> j t p", t=PACK), gate_col[:, n : n + 1], sig[n][:],
+                m, acc[:].rearrange("j (p t) -> j t p", t=PACK), gate_col[:, n : n + 1], sig[:, n, :, :],
                 ALU.mult, ALU.mult,
             )
             turned[n] = psum_turn.tile([P, PACK, P], F32, name="turned")
@@ -169,16 +171,14 @@ def tile_moe_bdx_glu_silu_kernel(
 
         def make_da(e, g, w):
             if (g, w) == (0, 1):
-                da_sb[e] = shared.tile(
-                    [P, G, 2, P * PACK], BF16, name="da_%d" % e, offset=slot_bytes * ((e + 2) % 3), align_bytes=64
-                )
+                da_sb[e] = ring.tile([P, G, 2, P * PACK], BF16, name="da", align_bytes=64)
                 codes[e] = ring.tile([P, G, 2, P], U32, name="codes", align_bytes=64)
                 scales[e] = ring.tile([P, G, 2, P], U8, name="scales", align_bytes=64)
-            factor = (y_sb[e], a1_sb[e])[w]
+            factor = (y_sb[e][:, g, :, :], a1_sb[e][:, :, g * P : (g + 1) * P])[w]
             nc.vector.tensor_tensor(
                 da_sb[e][:, g, w, :].rearrange("p (c i t) -> p c t i", i=4, t=PACK),
                 turned[e * G + g][:].rearrange("p t (c i) -> p c t i", i=4),
-                factor[:, :, g * P : (g + 1) * P].rearrange("p t (c i) -> p c t i", i=4),
+                factor.rearrange("p t (c i) -> p c t i", i=4),
                 ALU.mult,
             )
 
@@ -189,68 +189,68 @@ def tile_moe_bdx_glu_silu_kernel(
                 in_=da_sb[e][:, g0:g1, :, :].rearrange("p g w j -> p (g w j)"),
             )
 
-        def second_product(e, g0, g1):
-            for kt in range(KT):
-                acc = psum_dx.tile([P, (g1 - g0) * P], F32, name="acc_dx")
+        def second_product(e, g0, g1, kt0, kt1, banks, tag):
+            acc = banks.tile([P, kt1 - kt0, (g1 - g0) * P], F32, name="acc_dx", tag=tag)
+            for kt in range(kt0, kt1):
                 for g in range(g0, g1):
                     for w, (words, plane) in enumerate(((w1_w, w1_s), (w3_w, w3_s))):
                         nc.tensor.matmul_mx(
-                            out=acc[:, (g - g0) * P : (g - g0 + 1) * P],
+                            out=acc[:, kt - kt0, (g - g0) * P : (g - g0 + 1) * P],
                             lhsT=words[:, e, 2 * kt * P : 2 * (kt + 1) * P].bitcast(FP4X4),
                             lhsT_scale=plane[:, e, kt * P : (kt + 1) * P],
                             rhs=codes[e][:, g, w, :].bitcast(FP8X4),
                             rhs_scale=scales[e][:, g, w, :],
                             start=(w == 0), stop=(w == 1),
                         )
-                nc.scalar.copy(dx[kt][:, e * C + g0 * P : e * C + g1 * P], acc[:])
+            return dx[:, kt0:kt1, e * C + g0 * P : e * C + g1 * P], acc[:]
 
-        for j in range(0, S, 2 * C):
-            gather_words(j, j + 2 * C)
-            gather_bytes(j, j + 2 * C)
-        make_one_less(0)
+        for gather in (gather_words, gather_bytes):
+            for j0, j1 in ((0, 2 * C), (2 * C, 4 * C), (4 * C, 5 * C)):
+                gather(j0, j1)
+        make_neg(0)
         make_y(0)
         make_sigmoid(0)
-        make_sigmoid(1)
-        make_one_less(1)
+        make_neg(1)
         make_y(1)
+        make_sigmoid(1)
         first_product(0)
-        make_sigmoid(2)
-        for e in range(E):
-            last = e == E - 1
-            n = e * G
-            first_product(n + 1)
-            if e > 0:
-                quantize(e - 1, 0, G)
-                if e + 1 < E:
-                    make_y(e + 1)
-                second_product(e - 1, 0, G)
-            if n + 3 < E * G:
-                make_sigmoid(n + 3)
-            if e + 2 < E:
-                make_one_less(e + 2)
-            make_da(e, 0, 1)
-            make_da(e, 0, 0)
-            if not last:
+        first_product(1)
+        gather_words(S - C, S)
+        gather_bytes(S - C, S)
+        for n in range(E * G):
+            e, g = divmod(n, G)
+            make_da(e, g, 1)
+            if n + 2 < E * G:
                 first_product(n + 2)
-            if n + 4 < E * G:
-                make_sigmoid(n + 4)
-            make_da(e, 1, 1)
-            if last:
+            if g == 0:
+                if e > 0:
+                    quantize(e - 1, 0, G)
+                    if e + 1 < E:
+                        make_y(e + 1)
+                if e + 2 < E:
+                    make_neg(e + 2)
+                if e > 0:
+                    pending = second_product(e - 1, 0, G, 0, KT, psum_dx, "acc_dx")
+                if e + 2 < E:
+                    make_sigmoid(e + 2)
+                if e > 0:
+                    nc.scalar.copy(*pending)
+            elif e == E - 1:
                 quantize(e, 0, 1)
-                second_product(e, 0, 1)
-            make_da(e, 1, 0)
+                nc.scalar.copy(*second_product(e, 0, 1, 0, KT, psum_dx, "acc_dx"))
+            make_da(e, g, 0)
         quantize(E - 1, 1, G)
-        second_product(E - 1, 1, G)
+        nc.scalar.copy(*second_product(E - 1, 1, G, 0, KT, psum_a1, "a1_t"))
 
         for kt in range(KT):
             first = keep.tile([P, T], F32, name="first_%d" % kt)
             second = keep.tile([P, T], F32, name="second_%d" % kt)
             total = keep.tile([P, T], F32, name="total_%d" % kt)
-            pieces = ((0, T),) if kt < KT - 1 else ((0, 512), (512, T))
+            pieces = ((0, T),) if kt < KT - 1 else ((0, 480), (480, T))
             for t0, t1 in pieces:
                 cols = slice(t0, t1)
-                nc.vector.tensor_copy(first[:, cols], dx[kt][:].indirect(pos1_sb[:, t0 // 16 : t1 // 16]))
-                nc.vector.tensor_copy(second[:, cols], dx[kt][:].indirect(pos2_sb[:, t0 // 16 : t1 // 16]))
-                adder = nc.vector if (kt, t1) == (KT - 1, T) else nc.gpsimd
+                nc.vector.tensor_copy(first[:, cols], dx[:, kt, :].indirect(pos1_sb[:, t0 // 16 : t1 // 16]))
+                nc.vector.tensor_copy(second[:, cols], dx[:, kt, :].indirect(pos2_sb[:, t0 // 16 : t1 // 16]))
+                adder, queue = (nc.vector, nc.scalar) if (kt, t1) == (KT - 1, T) else (nc.gpsimd, nc.sync)
                 adder.tensor_tensor(total[:, cols], first[:, cols], second[:, cols], ALU.add)
-                nc.sync.dma_start(out=out[kt * P : (kt + 1) * P, cols], in_=total[:, cols])
+                queue.dma_start(out=out[kt * P : (kt + 1) * P, cols], in_=total[:, cols])

@@ -58,8 +58,8 @@ def tile_moe_bdx_glu_silu_kernel(
         a3_sb = [keep.tile([P, PACK, C], F32, name="a3_%d" % e) for e in range(E)]
         dx = keep.tile([P, KT, S], F32, name="dx")
 
+        nc.gpsimd.memset(dy_s[:].bitcast(I32), 0)
         make_identity(nc, ident[:])
-        nc.vector.memset(dy_s[:].bitcast(I32), 0)
         nc.vector.memset(w2_s[:].bitcast(I32), 0)
         nc.vector.memset(w1_s[:].bitcast(I32), 0)
         nc.vector.memset(w3_s[:].bitcast(I32), 0)
@@ -82,30 +82,30 @@ def tile_moe_bdx_glu_silu_kernel(
                 out=tile[:], in_=src[:, e * C : (e + 1) * C].rearrange("(p t) c -> p t c", t=PACK)
             )
 
-        nc.sync.dma_start(out=dy_w[:], in_=dy_words[0].rearrange("p t d -> p (t d)").bitcast(I32))
         nc.sync.dma_start(offs_sb[:], offs)
         for quad in range(4):
             nc.sync.dma_start(
                 out=dy_s[32 * quad : 32 * quad + 4, :].bitcast(I32),
                 in_=dy_scales[0, 4 * quad : 4 * quad + 4, :].bitcast(I32),
             )
-        nc.sync.dma_start(out=gate_rows[:], in_=gate.rearrange("h (g p) -> (h g) p", p=P)[0:P, :])
         load_saved(a1_sb[0], a1, 0)
+        nc.sync.dma_start(out=dy_w[:], in_=dy_words[0].rearrange("p t d -> p (t d)").bitcast(I32))
         load_scales(nc.sync, w2_s, w2_scales, range(4))
+        nc.sync.dma_start(out=gate_rows[:], in_=gate.rearrange("h (g p) -> (h g) p", p=P)[0:P, :])
+        load_saved(a3_sb[0], a3, 0)
         load_saved(a1_sb[1], a1, 1)
         load_words(w2_w, w2_words, 0, 2)
-        load_saved(a3_sb[0], a3, 0)
         load_saved(a1_sb[2], a1, 2)
-        load_words(w2_w, w2_words, 2, 6)
         load_saved(a3_sb[1], a3, 1)
-        load_saved(a1_sb[3], a1, 3)
         load_saved(a3_sb[2], a3, 2)
-        load_saved(a1_sb[4], a1, 4)
+        load_words(w2_w, w2_words, 2, 6)
+        load_saved(a1_sb[3], a1, 3)
         load_scales(nc.sync, w1_s, w1_scales, range(4))
+        load_saved(a1_sb[4], a1, 4)
         load_saved(a3_sb[3], a3, 3)
         load_saved(a1_sb[5], a1, 5)
-        load_scales(nc.sync, w3_s, w3_scales, range(4))
         load_words(w1_w, w1_words, 0, 6)
+        load_scales(nc.sync, w3_s, w3_scales, range(4))
         load_words(w3_w, w3_words, 0, 6)
         load_saved(a3_sb[4], a3, 4)
         load_saved(a3_sb[5], a3, 5)
@@ -128,15 +128,20 @@ def tile_moe_bdx_glu_silu_kernel(
         def make_neg(e):
             neg[e] = ring.tile([P, PACK, C], F32, name="neg")
             nc.scalar.activation(neg[e][:], a1_sb[e][:], ACT.Silu, scale=-1.0)
-
-        def make_y(e):
             if e < 2:
                 y_sb[e] = keep.tile([P, G, PACK, P], F32, name="y_%d" % e)[:]
             else:
                 y_sb[e] = sig[:, e * G - 1 : e * G + 1, :, :]
-            by_row = y_sb[e].rearrange("p g t j -> p t g j")
-            nc.gpsimd.tensor_scalar(by_row, neg[e][:].rearrange("p t (g j) -> p t g j", g=G), -1.0, 1.0, ALU.mult, ALU.add)
-            nc.gpsimd.tensor_tensor(by_row, by_row, a3_sb[e][:].rearrange("p t (g j) -> p t g j", g=G), ALU.mult)
+                nc.scalar.activation(neg[e][:, :, 0:P], neg[e][:, :, 0:P], ACT.Identity, bias=1.0, scale=-1.0)
+
+        def make_y(e, g0, g1):
+            by_row = y_sb[e][:, g0:g1, :, :].rearrange("p g t j -> p t g j")
+            cols = slice(g0 * P, g1 * P)
+            factor = neg[e][:, :, cols].rearrange("p t (g j) -> p t g j", j=P)
+            if e < 2 or g0 > 0:
+                nc.gpsimd.tensor_scalar(by_row, factor, -1.0, 1.0, ALU.mult, ALU.add)
+                factor = by_row
+            nc.gpsimd.tensor_tensor(by_row, factor, a3_sb[e][:, :, cols].rearrange("p t (g j) -> p t g j", j=P), ALU.mult)
 
         def make_sigmoid(e):
             th = []
@@ -171,9 +176,9 @@ def tile_moe_bdx_glu_silu_kernel(
 
         def make_da(e, g, w):
             if (g, w) == (0, 1):
-                da_sb[e] = ring.tile([P, G, 2, P * PACK], BF16, name="da", align_bytes=64)
-                codes[e] = ring.tile([P, G, 2, P], U32, name="codes", align_bytes=64)
-                scales[e] = ring.tile([P, G, 2, P], U8, name="scales", align_bytes=64)
+                da_sb[e] = keep.tile([P, G, 2, P * PACK], BF16, name="da_%d" % e, align_bytes=64)
+                codes[e] = keep.tile([P, G, 2, P], U32, name="codes_%d" % e, align_bytes=64)
+                scales[e] = keep.tile([P, G, 2, P], U8, name="scales_%d" % e, align_bytes=64)
             factor = (y_sb[e][:, g, :, :], a1_sb[e][:, :, g * P : (g + 1) * P])[w]
             nc.vector.tensor_tensor(
                 da_sb[e][:, g, w, :].rearrange("p (c i t) -> p c t i", i=4, t=PACK),
@@ -204,14 +209,14 @@ def tile_moe_bdx_glu_silu_kernel(
                         )
             return dx[:, kt0:kt1, e * C + g0 * P : e * C + g1 * P], acc[:]
 
-        for gather in (gather_words, gather_bytes):
+        for gather in (gather_bytes, gather_words):
             for j0, j1 in ((0, 2 * C), (2 * C, 4 * C), (4 * C, 5 * C)):
                 gather(j0, j1)
         make_neg(0)
-        make_y(0)
+        make_y(0, 0, G)
         make_sigmoid(0)
         make_neg(1)
-        make_y(1)
+        make_y(1, 0, G)
         make_sigmoid(1)
         first_product(0)
         first_product(1)
@@ -226,7 +231,7 @@ def tile_moe_bdx_glu_silu_kernel(
                 if e > 0:
                     quantize(e - 1, 0, G)
                     if e + 1 < E:
-                        make_y(e + 1)
+                        make_y(e + 1, 1, G)
                 if e + 2 < E:
                     make_neg(e + 2)
                 if e > 0:
@@ -235,12 +240,16 @@ def tile_moe_bdx_glu_silu_kernel(
                     make_sigmoid(e + 2)
                 if e > 0:
                     nc.scalar.copy(*pending)
+            elif e + 2 < E:
+                make_y(e + 2, 0, 1)
             elif e == E - 1:
                 quantize(e, 0, 1)
-                nc.scalar.copy(*second_product(e, 0, 1, 0, KT, psum_dx, "acc_dx"))
+                for kt in range(KT):
+                    nc.scalar.copy(*second_product(e, 0, 1, kt, kt + 1, psum_a1, "a1_t"))
             make_da(e, g, 0)
         quantize(E - 1, 1, G)
-        nc.scalar.copy(*second_product(E - 1, 1, G, 0, KT, psum_a1, "a1_t"))
+        for kt in range(KT):
+            nc.scalar.copy(*second_product(E - 1, 1, G, kt, kt + 1, psum_a1, "a1_t"))
 
         for kt in range(KT):
             first = keep.tile([P, T], F32, name="first_%d" % kt)

@@ -33,10 +33,9 @@ def tile_moe_bdx_glu_silu_kernel(
     with ExitStack() as ctx:
         keep = ctx.enter_context(tc.tile_pool(name="keep", bufs=1))
         ring = ctx.enter_context(tc.tile_pool(name="ring", bufs=3))
-        psum_a1 = ctx.enter_context(tc.psum_pool(name="psum_a1", bufs=2))
+        psum_a1 = ctx.enter_context(tc.psum_pool(name="psum_a1", bufs=3))
         psum_dh = ctx.enter_context(tc.psum_pool(name="psum_dh", bufs=2))
         psum_turn = ctx.enter_context(tc.psum_pool(name="psum_turn", bufs=3))
-        psum_dx = ctx.enter_context(tc.psum_pool(name="psum_dx", bufs=1))
 
         offs_sb = keep.tile([P, S // 16], U16, name="offs_sb")
         pos1_sb = keep.tile([P, T // 16], U16, name="pos1_sb")
@@ -51,24 +50,24 @@ def tile_moe_bdx_glu_silu_kernel(
         w2_s = keep.tile([P, E, H], U8, name="w2_s", align_bytes=64)
         w1_s = keep.tile([P, E, K], U8, name="w1_s", align_bytes=64)
         w3_s = keep.tile([P, E, K], U8, name="w3_s", align_bytes=64)
-        gate_rows = keep.tile([P, P], F32, name="gate_rows")
+        gate_rows = keep.tile([P, S // PACK], F32, name="gate_rows")
         gate_col = keep.tile([P, E * G], F32, name="gate_col")
         ident = keep.tile([P, P], F32, name="ident")
-        a1_sb = [keep.tile([P, PACK, C], F32, name="a1_%d" % e) for e in range(E)]
-        a3_sb = [keep.tile([P, PACK, C], F32, name="a3_%d" % e) for e in range(E)]
+        a1_sb, a3_sb = {}, {}
         dx = keep.tile([P, KT, S], F32, name="dx")
 
         nc.gpsimd.memset(dy_s[:].bitcast(I32), 0)
+        nc.gpsimd.memset(gate_rows[:], 0.0)
         make_identity(nc, ident[:])
         nc.vector.memset(w2_s[:].bitcast(I32), 0)
         nc.vector.memset(w1_s[:].bitcast(I32), 0)
         nc.vector.memset(w3_s[:].bitcast(I32), 0)
 
-        def load_scales(queue, plane, src, quads):
-            for quad in quads:
-                queue.dma_start(
-                    out=plane[32 * quad : 32 * quad + 4, :, :].bitcast(I32),
-                    in_=src[:, 0, 4 * quad : 4 * quad + 4, :].rearrange("e r i -> r e i").bitcast(I32),
+        def load_scales(plane, src):
+            for r in range(4):
+                nc.sync.dma_start(
+                    out=plane[r:P:32, :, :].bitcast(I32),
+                    in_=src[:, 0, r:16:4, :].rearrange("e q i -> q e i").bitcast(I32),
                 )
 
         def load_words(tile, src, e0, e1):
@@ -77,44 +76,42 @@ def tile_moe_bdx_glu_silu_kernel(
                 in_=src[e0:e1, 0, :, :].rearrange("e p b -> p e b").bitcast(I32),
             )
 
-        def load_saved(tile, src, e):
-            nc.sync.dma_start(
-                out=tile[:], in_=src[:, e * C : (e + 1) * C].rearrange("(p t) c -> p t c", t=PACK)
-            )
+        def load_saved(views, src, name, e0, e1):
+            tile = keep.tile([P, PACK, (e1 - e0) * C], F32, name="%s_%d" % (name, e0))
+            nc.sync.dma_start(out=tile[:], in_=src[:, e0 * C : e1 * C].rearrange("(p t) c -> p t c", t=PACK))
+            for e in range(e0, e1):
+                views[e] = tile[:, :, (e - e0) * C : (e - e0 + 1) * C]
 
         nc.sync.dma_start(offs_sb[:], offs)
-        for quad in range(4):
-            nc.sync.dma_start(
-                out=dy_s[32 * quad : 32 * quad + 4, :].bitcast(I32),
-                in_=dy_scales[0, 4 * quad : 4 * quad + 4, :].bitcast(I32),
-            )
-        load_saved(a1_sb[0], a1, 0)
+        for r in range(4):
+            nc.sync.dma_start(out=dy_s[r:P:32, :].bitcast(I32), in_=dy_scales[0, r:16:4, :].bitcast(I32))
+        nc.sync.dma_start(out=gate_rows[0:PACK, :], in_=gate[0, :].rearrange("(r c) -> r c", r=PACK))
+        load_saved(a1_sb, a1, "a1", 0, 1)
         nc.sync.dma_start(out=dy_w[:], in_=dy_words[0].rearrange("p t d -> p (t d)").bitcast(I32))
-        load_scales(nc.sync, w2_s, w2_scales, range(4))
-        nc.sync.dma_start(out=gate_rows[:], in_=gate.rearrange("h (g p) -> (h g) p", p=P)[0:P, :])
-        load_saved(a3_sb[0], a3, 0)
-        load_saved(a1_sb[1], a1, 1)
         load_words(w2_w, w2_words, 0, 2)
-        load_saved(a1_sb[2], a1, 2)
-        load_saved(a3_sb[1], a3, 1)
-        load_saved(a3_sb[2], a3, 2)
-        load_words(w2_w, w2_words, 2, 6)
-        load_saved(a1_sb[3], a1, 3)
-        load_scales(nc.sync, w1_s, w1_scales, range(4))
-        load_saved(a1_sb[4], a1, 4)
-        load_saved(a3_sb[3], a3, 3)
-        load_saved(a1_sb[5], a1, 5)
+        load_scales(w2_s, w2_scales)
+        load_saved(a1_sb, a1, "a1", 1, 2)
+        load_saved(a3_sb, a3, "a3", 0, 1)
+        load_saved(a1_sb, a1, "a1", 2, 4)
+        load_words(w2_w, w2_words, 2, 4)
+        load_saved(a3_sb, a3, "a3", 1, 2)
+        load_saved(a3_sb, a3, "a3", 2, 4)
+        load_saved(a1_sb, a1, "a1", 4, 6)
+        load_words(w2_w, w2_words, 4, 6)
+        load_scales(w1_s, w1_scales)
+        load_scales(w3_s, w3_scales)
         load_words(w1_w, w1_words, 0, 6)
-        load_scales(nc.sync, w3_s, w3_scales, range(4))
         load_words(w3_w, w3_words, 0, 6)
-        load_saved(a3_sb[4], a3, 4)
-        load_saved(a3_sb[5], a3, 5)
+        load_saved(a3_sb, a3, "a3", 4, 5)
+        load_saved(a3_sb, a3, "a3", 5, 6)
         nc.sync.dma_start(pos1_sb[:], pos1)
         nc.sync.dma_start(pos2_sb[:], pos2)
 
-        gate_ps = psum_dx.tile([P, P], F32, name="gate_ps", tag="acc_dx")
-        nc.tensor.transpose(gate_ps[:], gate_rows[:], ident[:])
-        nc.scalar.copy(gate_col[:], gate_ps[:, 0 : E * G])
+        blocks = S // PACK // P
+        gate_ps = psum_a1.tile([P, blocks, P], F32, name="gate_ps", tag="a1_t")
+        for b in range(blocks):
+            nc.tensor.transpose(gate_ps[:, b, :], gate_rows[:, b * P : (b + 1) * P], ident[:])
+        nc.scalar.copy(gate_col[:].rearrange("p (r b) -> p r b", b=blocks), gate_ps[:, :, 0:PACK].rearrange("p b r -> p r b"))
 
         def gather_words(j0, j1):
             nc.vector.tensor_copy(g_w[:, j0 % (S - C) : j0 % (S - C) + j1 - j0], dy_w[:].bitcast(U32).indirect(offs_sb[:, j0 // 16 : j1 // 16]))
@@ -127,7 +124,7 @@ def tile_moe_bdx_glu_silu_kernel(
 
         def make_neg(e):
             neg[e] = ring.tile([P, PACK, C], F32, name="neg")
-            nc.scalar.activation(neg[e][:], a1_sb[e][:], ACT.Silu, scale=-1.0)
+            nc.scalar.activation(neg[e][:], a1_sb[e], ACT.Silu, scale=-1.0)
             if e < 2:
                 y_sb[e] = keep.tile([P, G, PACK, P], F32, name="y_%d" % e)[:]
             else:
@@ -194,8 +191,8 @@ def tile_moe_bdx_glu_silu_kernel(
                 in_=da_sb[e][:, g0:g1, :, :].rearrange("p g w j -> p (g w j)"),
             )
 
-        def second_product(e, g0, g1, kt0, kt1, banks, tag):
-            acc = banks.tile([P, kt1 - kt0, (g1 - g0) * P], F32, name="acc_dx", tag=tag)
+        def second_product(e, g0, g1, kt0, kt1):
+            acc = psum_a1.tile([P, kt1 - kt0, (g1 - g0) * P], F32, name="acc_dx", tag="a1_t")
             for kt in range(kt0, kt1):
                 for g in range(g0, g1):
                     for w, (words, plane) in enumerate(((w1_w, w1_s), (w3_w, w3_s))):
@@ -207,7 +204,7 @@ def tile_moe_bdx_glu_silu_kernel(
                             rhs_scale=scales[e][:, g, w, :],
                             start=(w == 0), stop=(w == 1),
                         )
-            return dx[:, kt0:kt1, e * C + g0 * P : e * C + g1 * P], acc[:]
+            nc.scalar.copy(dx[:, kt0:kt1, e * C + g0 * P : e * C + g1 * P], acc[:])
 
         for gather in (gather_bytes, gather_words):
             for j0, j1 in ((0, 2 * C), (2 * C, 4 * C), (4 * C, 5 * C)):
@@ -234,22 +231,33 @@ def tile_moe_bdx_glu_silu_kernel(
                         make_y(e + 1, 1, G)
                 if e + 2 < E:
                     make_neg(e + 2)
-                if e > 0:
-                    pending = second_product(e - 1, 0, G, 0, KT, psum_dx, "acc_dx")
-                if e + 2 < E:
                     make_sigmoid(e + 2)
-                if e > 0:
-                    nc.scalar.copy(*pending)
             elif e + 2 < E:
                 make_y(e + 2, 0, 1)
             elif e == E - 1:
                 quantize(e, 0, 1)
                 for kt in range(KT):
-                    nc.scalar.copy(*second_product(e, 0, 1, kt, kt + 1, psum_a1, "a1_t"))
+                    second_product(e, 0, 1, kt, kt + 1)
+            if 6 <= n < 11:
+                second_product(n - 6, 0, G, 0, KT)
             make_da(e, g, 0)
-        quantize(E - 1, 1, G)
+        last = [psum_a1.tile([P, P], F32, name="acc_last", tag="a1_t") for kt in range(KT)]
+        for w, (words, plane) in ((1, (w3_w, w3_s)), (0, (w1_w, w1_s))):
+            nc.vector.quantize_mx(
+                out=codes[E - 1][:, G - 1, w, :].bitcast(FP8X4), scales=scales[E - 1][:, G - 1, w, :],
+                in_=da_sb[E - 1][:, G - 1, w, :],
+            )
+            for kt in range(KT):
+                nc.tensor.matmul_mx(
+                    out=last[kt][:],
+                    lhsT=words[:, E - 1, 2 * kt * P : 2 * (kt + 1) * P].bitcast(FP4X4),
+                    lhsT_scale=plane[:, E - 1, kt * P : (kt + 1) * P],
+                    rhs=codes[E - 1][:, G - 1, w, :].bitcast(FP8X4),
+                    rhs_scale=scales[E - 1][:, G - 1, w, :],
+                    start=(w == 1), stop=(w == 0),
+                )
         for kt in range(KT):
-            nc.scalar.copy(*second_product(E - 1, 1, G, kt, kt + 1, psum_a1, "a1_t"))
+            nc.scalar.copy(dx[:, kt, S - P : S], last[kt][:])
 
         for kt in range(KT):
             first = keep.tile([P, T], F32, name="first_%d" % kt)

@@ -54,7 +54,7 @@ def tile_moe_bdx_glu_silu_kernel(
         gate_col = keep.tile([P, E * G], F32, name="gate_col")
         ident = keep.tile([P, P], F32, name="ident")
         a1_sb, a3_sb = {}, {}
-        dx = keep.tile([P, KT, S], F32, name="dx")
+        dx = [keep.tile([P, S], F32, name="dx_%d" % kt) for kt in range(KT)]
 
         nc.gpsimd.memset(dy_s[:].bitcast(I32), 0)
         nc.gpsimd.memset(gate_rows[:], 0.0)
@@ -204,7 +204,8 @@ def tile_moe_bdx_glu_silu_kernel(
                             rhs_scale=scales[e][:, g, w, :],
                             start=(w == 0), stop=(w == 1),
                         )
-            nc.scalar.copy(dx[:, kt0:kt1, e * C + g0 * P : e * C + g1 * P], acc[:])
+            for kt in range(kt0, kt1):
+                nc.scalar.copy(dx[kt][:, e * C + g0 * P : e * C + g1 * P], acc[:, kt - kt0, :])
 
         for gather in (gather_bytes, gather_words):
             for j0, j1 in ((0, 2 * C), (2 * C, 4 * C), (4 * C, 5 * C)):
@@ -257,17 +258,14 @@ def tile_moe_bdx_glu_silu_kernel(
                     start=(w == 1), stop=(w == 0),
                 )
         for kt in range(KT):
-            nc.scalar.copy(dx[:, kt, S - P : S], last[kt][:])
+            nc.scalar.copy(dx[kt][:, S - P : S], last[kt][:])
 
+        first = [keep.tile([P, T], F32, name="first_%d" % kt) for kt in range(KT)]
+        total = [keep.tile([P, T], F32, name="total_%d" % kt) for kt in range(KT)]
         for kt in range(KT):
-            first = keep.tile([P, T], F32, name="first_%d" % kt)
-            second = keep.tile([P, T], F32, name="second_%d" % kt)
-            total = keep.tile([P, T], F32, name="total_%d" % kt)
-            pieces = ((0, T),) if kt < KT - 1 else ((0, 480), (480, T))
-            for t0, t1 in pieces:
-                cols = slice(t0, t1)
-                nc.vector.tensor_copy(first[:, cols], dx[:, kt, :].indirect(pos1_sb[:, t0 // 16 : t1 // 16]))
-                nc.vector.tensor_copy(second[:, cols], dx[:, kt, :].indirect(pos2_sb[:, t0 // 16 : t1 // 16]))
-                adder, queue = (nc.vector, nc.scalar) if (kt, t1) == (KT - 1, T) else (nc.gpsimd, nc.sync)
-                adder.tensor_tensor(total[:, cols], first[:, cols], second[:, cols], ALU.add)
-                queue.dma_start(out=out[kt * P : (kt + 1) * P, cols], in_=total[:, cols])
+            nc.vector.tensor_copy(first[kt][:], dx[kt][:].indirect(pos1_sb[:]))
+        for kt, t0, t1, queue in ((0, 0, T, nc.sync), (1, 0, 512, nc.sync), (1, 512, T, nc.scalar)):
+            nc.vector.tensor_tensor(
+                total[kt][:, t0:t1], dx[kt][:].indirect(pos2_sb[:, t0 // 16 : t1 // 16]), first[kt][:, t0:t1], ALU.add
+            )
+            queue.dma_start(out=out[kt * P : (kt + 1) * P, t0:t1], in_=total[kt][:, t0:t1])

@@ -9,6 +9,8 @@ P = 128
 PACK = 4
 G = C // P
 KT = K // P
+TURN_BANKS = 4
+RUN = 4
 
 FLOPS = 2 * S * (N * H + 2 * H * K)
 BYTES = 4 * (2 * H * S + S + K * T) + (N * T + N * T // 32) + E * (N * H + 2 * H * K) * 17 // 32 + 2 * P * (S + 2 * T) // 16
@@ -33,9 +35,10 @@ def tile_moe_bdx_glu_silu_kernel(
     with ExitStack() as ctx:
         keep = ctx.enter_context(tc.tile_pool(name="keep", bufs=1))
         ring = ctx.enter_context(tc.tile_pool(name="ring", bufs=3))
-        psum_a1 = ctx.enter_context(tc.psum_pool(name="psum_a1", bufs=3))
-        psum_dh = ctx.enter_context(tc.psum_pool(name="psum_dh", bufs=2))
-        psum_turn = ctx.enter_context(tc.psum_pool(name="psum_turn", bufs=3))
+        psum = ctx.enter_context(tc.psum_pool(name="psum", bufs=1))
+        sum_banks = [psum.tile([P, H], F32, name="sum_bank_%d" % b) for b in range(2)]
+        turn_banks = [psum.tile([P, PACK, P], F32, name="turn_bank_%d" % b) for b in range(TURN_BANKS)]
+        dx_banks = [psum.tile([P, PACK, P], F32, name="dx_bank_%d" % b) for b in range(2)]
 
         offs_sb = keep.tile([P, S // 16], U16, name="offs_sb")
         pos1_sb = keep.tile([P, T // 16], U16, name="pos1_sb")
@@ -54,7 +57,6 @@ def tile_moe_bdx_glu_silu_kernel(
         gate_col = keep.tile([P, E * G], F32, name="gate_col")
         ident = keep.tile([P, P], F32, name="ident")
         a1_sb, a3_sb = {}, {}
-        dx = [keep.tile([P, S], F32, name="dx_%d" % kt) for kt in range(KT)]
 
         nc.gpsimd.memset(dy_s[:].bitcast(I32), 0)
         nc.gpsimd.memset(gate_rows[:], 0.0)
@@ -88,30 +90,27 @@ def tile_moe_bdx_glu_silu_kernel(
         nc.sync.dma_start(out=gate_rows[0:PACK, :], in_=gate[0, :].rearrange("(r c) -> r c", r=PACK))
         load_saved(a1_sb, a1, "a1", 0, 1)
         nc.sync.dma_start(out=dy_w[:], in_=dy_words[0].rearrange("p t d -> p (t d)").bitcast(I32))
+        load_saved(a1_sb, a1, "a1", 1, 2)
         load_words(w2_w, w2_words, 0, 2)
         load_scales(w2_s, w2_scales)
-        load_saved(a1_sb, a1, "a1", 1, 2)
         load_saved(a3_sb, a3, "a3", 0, 1)
-        load_saved(a1_sb, a1, "a1", 2, 4)
-        load_words(w2_w, w2_words, 2, 4)
-        load_saved(a3_sb, a3, "a3", 1, 2)
-        load_saved(a3_sb, a3, "a3", 2, 4)
-        load_saved(a1_sb, a1, "a1", 4, 6)
-        load_words(w2_w, w2_words, 4, 6)
+        for e in range(2, E):
+            load_saved(a1_sb, a1, "a1", e, e + 1)
+            if e % 2 == 0:
+                load_words(w2_w, w2_words, e, e + 2)
+            load_saved(a3_sb, a3, "a3", e - 1, e)
         load_scales(w1_s, w1_scales)
+        load_saved(a3_sb, a3, "a3", E - 1, E)
         load_scales(w3_s, w3_scales)
-        load_words(w1_w, w1_words, 0, 6)
-        load_words(w3_w, w3_words, 0, 6)
-        load_saved(a3_sb, a3, "a3", 4, 5)
-        load_saved(a3_sb, a3, "a3", 5, 6)
+        load_words(w1_w, w1_words, 0, E)
+        load_words(w3_w, w3_words, 0, E)
         nc.sync.dma_start(pos1_sb[:], pos1)
         nc.sync.dma_start(pos2_sb[:], pos2)
 
         blocks = S // PACK // P
-        gate_ps = psum_a1.tile([P, blocks, P], F32, name="gate_ps", tag="a1_t")
         for b in range(blocks):
-            nc.tensor.transpose(gate_ps[:, b, :], gate_rows[:, b * P : (b + 1) * P], ident[:])
-        nc.scalar.copy(gate_col[:].rearrange("p (r b) -> p r b", b=blocks), gate_ps[:, :, 0:PACK].rearrange("p b r -> p r b"))
+            nc.tensor.transpose(dx_banks[0][:, b, :], gate_rows[:, b * P : (b + 1) * P], ident[:])
+        nc.scalar.copy(gate_col[:].rearrange("p (r b) -> p r b", b=blocks), dx_banks[0][:, 0:blocks, 0:PACK].rearrange("p b r -> p r b"))
 
         def gather_words(j0, j1):
             nc.vector.tensor_copy(g_w[:, j0 % (S - C) : j0 % (S - C) + j1 - j0], dy_w[:].bitcast(U32).indirect(offs_sb[:, j0 // 16 : j1 // 16]))
@@ -119,146 +118,143 @@ def tile_moe_bdx_glu_silu_kernel(
         def gather_bytes(j0, j1):
             nc.vector.tensor_copy(g_s[:, j0 % (S - C) : j0 % (S - C) + j1 - j0], dy_s[:].indirect(offs_sb[:, j0 // 16 : j1 // 16]))
 
-        neg, y_sb, turned, da_sb, codes, scales = {}, {}, {}, {}, {}, {}
+        y_sb, da_sb, codes, scales = {}, {}, {}, {}
         sig = keep.tile([P, E * G, PACK, P], F32, name="sig")
+        th = [keep.tile([P, G, PACK, P], F32, name="th_%d" % e) for e in range(E - 1)]
+        th.append(keep.tile([P, G, PACK, P], F32, name="th_last", tag="dx_1"))
+        neg = [keep.tile([P, G, PACK, P], F32, name="neg_0")] + th[1 : E - 1]
+        neg.append(keep.tile([P, G, PACK, P], F32, name="neg_last", tag="dx_0"))
+        rest_last = keep.tile([P, G, PACK, P], F32, name="rest_last")
+        dx = []
+
+        def by_group(saved, n):
+            return saved[n // G][:, :, n % G * P : (n % G + 1) * P]
 
         def make_neg(e):
-            neg[e] = ring.tile([P, PACK, C], F32, name="neg")
-            nc.scalar.activation(neg[e][:], a1_sb[e], ACT.Silu, scale=-1.0)
-            if e < 2:
-                y_sb[e] = keep.tile([P, G, PACK, P], F32, name="y_%d" % e)[:]
-            else:
-                y_sb[e] = sig[:, e * G - 1 : e * G + 1, :, :]
-                nc.scalar.activation(neg[e][:, :, 0:P], neg[e][:, :, 0:P], ACT.Identity, bias=1.0, scale=-1.0)
+            nc.scalar.activation(neg[e][:], a1_sb[e].rearrange("p t (g j) -> p g t j", j=P), ACT.Silu, scale=-1.0)
+            if e == E - 1:
+                nc.scalar.activation(rest_last[:], neg[e][:], ACT.Identity, bias=1.0, scale=-1.0)
+            elif e >= 2:
+                nc.scalar.activation(neg[e][:, 1, :, :], neg[e][:, 1, :, :], ACT.Identity, bias=1.0, scale=-1.0)
 
-        def make_y(e, g0, g1):
-            by_row = y_sb[e][:, g0:g1, :, :].rearrange("p g t j -> p t g j")
-            cols = slice(g0 * P, g1 * P)
-            factor = neg[e][:, :, cols].rearrange("p t (g j) -> p t g j", j=P)
-            if e < 2 or g0 > 0:
-                nc.gpsimd.tensor_scalar(by_row, factor, -1.0, 1.0, ALU.mult, ALU.add)
-                factor = by_row
-            nc.gpsimd.tensor_tensor(by_row, factor, a3_sb[e][:, :, cols].rearrange("p t (g j) -> p t g j", j=P), ALU.mult)
+        def make_y(n):
+            e, g = divmod(n, G)
+            y_sb[n] = sig[:, n, :, :] if e >= 2 else keep.tile([P, PACK, P], F32, name="y_%d" % n)[:]
+            factor = (neg[e] if e < E - 1 else rest_last)[:, g, :, :]
+            if e < 2 or (g == 0 and e < E - 1):
+                nc.gpsimd.tensor_scalar(y_sb[n], factor, -1.0, 1.0, ALU.mult, ALU.add)
+                factor = y_sb[n]
+            nc.gpsimd.tensor_tensor(y_sb[n], factor, by_group(a3_sb, n), ALU.mult)
 
         def make_sigmoid(e):
-            th = []
             for g in range(G):
-                a1_t = psum_a1.tile([P, PACK, P], F32, name="a1_t")
+                a1_t = turn_banks[(e * G + g) % TURN_BANKS]
                 for t in range(PACK):
-                    nc.tensor.transpose(a1_t[:, t, :], a1_sb[e][:, t, g * P : (g + 1) * P], ident[:])
-                th.append(ring.tile([P, PACK, P], F32, name="th"))
-                nc.scalar.activation(th[g][:], a1_t[:], ACT.Tanh, scale=0.5)
-            for g in range(G):
-                nc.scalar.activation(sig[:, e * G + g, :, :], th[g][:], ACT.Identity, bias=0.5, scale=0.5)
+                    nc.tensor.transpose(a1_t[:, t, :], by_group(a1_sb, e * G + g)[:, t, :], ident[:])
+                nc.scalar.activation(th[e][:, g, :, :], a1_t[:], ACT.Tanh, scale=0.5)
+            nc.scalar.activation(sig[:, e * G : (e + 1) * G, :, :], th[e][:], ACT.Identity, bias=0.5, scale=0.5)
+
+        def turned(n):
+            return turn_banks[(n + 2) % TURN_BANKS] if n < 10 else dx_banks[n - 10]
 
         def first_product(n):
             e = n // G
             cols = slice(n * P % (S - C), n * P % (S - C) + P)
-            acc = psum_dh.tile([P, H], F32, name="acc")
+            acc = sum_banks[n % 2]
             nc.tensor.matmul_mx(
                 out=acc[:], lhsT=g_w[:, cols].bitcast(FP8X4), lhsT_scale=g_s[:, cols],
                 rhs=w2_w[:, e, :].bitcast(FP4X4), rhs_scale=w2_s[:, e, :], start=True, stop=True,
             )
-            if n < 3:
-                m = ring.tile([P, PACK, P], F32, name="m")[:]
-            else:
-                m = y_sb[(n - 3) // G][:, (n - 3) % G, :, :]
+            m = ring.tile([P, PACK, P], F32, name="m")[:] if n < 3 else y_sb[n - 3]
             nc.vector.scalar_tensor_tensor(
                 m, acc[:].rearrange("j (p t) -> j t p", t=PACK), gate_col[:, n : n + 1], sig[:, n, :, :],
                 ALU.mult, ALU.mult,
             )
-            turned[n] = psum_turn.tile([P, PACK, P], F32, name="turned")
             for t in range(PACK):
-                nc.tensor.transpose(turned[n][:, t, :], m[:, t, :], ident[:])
+                nc.tensor.transpose(turned(n)[:, t, :], m[:, t, :], ident[:])
 
-        def make_da(e, g, w):
+        def make_da(n, w):
+            e, g = divmod(n, G)
             if (g, w) == (0, 1):
                 da_sb[e] = keep.tile([P, G, 2, P * PACK], BF16, name="da_%d" % e, align_bytes=64)
                 codes[e] = keep.tile([P, G, 2, P], U32, name="codes_%d" % e, align_bytes=64)
                 scales[e] = keep.tile([P, G, 2, P], U8, name="scales_%d" % e, align_bytes=64)
-            factor = (y_sb[e][:, g, :, :], a1_sb[e][:, :, g * P : (g + 1) * P])[w]
+            factor = (y_sb[n], by_group(a1_sb, n))[w]
             nc.vector.tensor_tensor(
-                da_sb[e][:, g, w, :].rearrange("p (c i t) -> p c t i", i=4, t=PACK),
-                turned[e * G + g][:].rearrange("p t (c i) -> p c t i", i=4),
-                factor.rearrange("p t (c i) -> p c t i", i=4),
+                da_sb[e][:, g, w, :].rearrange("p (c i t) -> p c t i", i=RUN, t=PACK),
+                turned(n)[:].rearrange("p t (c i) -> p c t i", i=RUN),
+                factor.rearrange("p t (c i) -> p c t i", i=RUN),
                 ALU.mult,
             )
 
-        def quantize(e, g0, g1):
-            nc.vector.quantize_mx(
-                out=codes[e][:, g0:g1, :, :].rearrange("p g w j -> p (g w j)").bitcast(FP8X4),
-                scales=scales[e][:, g0:g1, :, :].rearrange("p g w j -> p (g w j)"),
-                in_=da_sb[e][:, g0:g1, :, :].rearrange("p g w j -> p (g w j)"),
+        def quantize(e, pick):
+            nc.vector.quantize_mx(out=pick(codes[e]).bitcast(FP8X4), scales=pick(scales[e]), in_=pick(da_sb[e]))
+
+        def second_pass(out_cols, n, kt, w, start, stop):
+            e, g = divmod(n, G)
+            words, plane = ((w1_w, w1_s), (w3_w, w3_s))[w]
+            nc.tensor.matmul_mx(
+                out=out_cols,
+                lhsT=words[:, e, 2 * kt * P : 2 * (kt + 1) * P].bitcast(FP4X4),
+                lhsT_scale=plane[:, e, kt * P : (kt + 1) * P],
+                rhs=codes[e][:, g, w, :].bitcast(FP8X4),
+                rhs_scale=scales[e][:, g, w, :],
+                start=start, stop=stop,
             )
 
-        def second_product(e, g0, g1, kt0, kt1):
-            acc = psum_a1.tile([P, kt1 - kt0, (g1 - g0) * P], F32, name="acc_dx", tag="a1_t")
-            for kt in range(kt0, kt1):
-                for g in range(g0, g1):
-                    for w, (words, plane) in enumerate(((w1_w, w1_s), (w3_w, w3_s))):
-                        nc.tensor.matmul_mx(
-                            out=acc[:, kt - kt0, (g - g0) * P : (g - g0 + 1) * P],
-                            lhsT=words[:, e, 2 * kt * P : 2 * (kt + 1) * P].bitcast(FP4X4),
-                            lhsT_scale=plane[:, e, kt * P : (kt + 1) * P],
-                            rhs=codes[e][:, g, w, :].bitcast(FP8X4),
-                            rhs_scale=scales[e][:, g, w, :],
-                            start=(w == 0), stop=(w == 1),
-                        )
-            for kt in range(kt0, kt1):
-                nc.scalar.copy(dx[kt][:, e * C + g0 * P : e * C + g1 * P], acc[:, kt - kt0, :])
+        def second_product(n0, n1, bank):
+            if not dx:
+                dx.extend(keep.tile([P, S], F32, name="dx_%d" % kt, tag="dx_%d" % kt) for kt in range(KT))
+            for kt in range(KT):
+                for n in range(n0, n1):
+                    for w in range(2):
+                        second_pass(bank[:, kt * G + n - n0, :], n, kt, w, w == 0, w == 1)
+            for kt in range(KT):
+                nc.scalar.copy(
+                    dx[kt][:, n0 * P : n1 * P].rearrange("p (g j) -> p g j", j=P), bank[:, kt * G : kt * G + n1 - n0, :]
+                )
 
         for gather in (gather_bytes, gather_words):
             for j0, j1 in ((0, 2 * C), (2 * C, 4 * C), (4 * C, 5 * C)):
                 gather(j0, j1)
         make_neg(0)
-        make_y(0, 0, G)
+        make_y(0)
+        make_y(1)
         make_sigmoid(0)
-        make_neg(1)
-        make_y(1, 0, G)
         make_sigmoid(1)
+        make_neg(1)
+        make_y(2)
+        make_y(3)
         first_product(0)
         first_product(1)
         gather_words(S - C, S)
         gather_bytes(S - C, S)
+        last = E * G - 1
         for n in range(E * G):
             e, g = divmod(n, G)
-            make_da(e, g, 1)
-            if n + 2 < E * G:
+            make_da(n, 1)
+            if g == 0 and e + 2 < E:
+                make_sigmoid(e + 2)
+                make_neg(e + 2)
+            if n + 2 <= last:
                 first_product(n + 2)
-            if g == 0:
-                if e > 0:
-                    quantize(e - 1, 0, G)
-                    if e + 1 < E:
-                        make_y(e + 1, 1, G)
-                if e + 2 < E:
-                    make_neg(e + 2)
-                    make_sigmoid(e + 2)
-            elif e + 2 < E:
-                make_y(e + 2, 0, 1)
-            elif e == E - 1:
-                quantize(e, 0, 1)
-                for kt in range(KT):
-                    second_product(e, 0, 1, kt, kt + 1)
-            if 6 <= n < 11:
-                second_product(n - 6, 0, G, 0, KT)
-            make_da(e, g, 0)
-        last = [psum_a1.tile([P, P], F32, name="acc_last", tag="a1_t") for kt in range(KT)]
-        for w, (words, plane) in ((1, (w3_w, w3_s)), (0, (w1_w, w1_s))):
-            nc.vector.quantize_mx(
-                out=codes[E - 1][:, G - 1, w, :].bitcast(FP8X4), scales=scales[E - 1][:, G - 1, w, :],
-                in_=da_sb[E - 1][:, G - 1, w, :],
-            )
+            if g == 0 and e > 0:
+                quantize(e - 1, lambda tile: tile[:].rearrange("p g w j -> p (g w j)"))
+            if 4 <= n + 2 <= last:
+                make_y(n + 2)
+            if n == last:
+                quantize(e, lambda tile: tile[:, 0, :, :].rearrange("p w j -> p (w j)"))
+                second_product(n - 1, n, turned(8))
+            make_da(n, 0)
+            if 6 <= n < last:
+                second_product((n - 6) * G, (n - 5) * G, (dx_banks + [turned(6), turned(7), turned(10)])[n - 6])
+        last_banks = (turned(9), turned(6))
+        for w in (1, 0):
+            quantize(E - 1, lambda tile: tile[:, G - 1, w, :])
             for kt in range(KT):
-                nc.tensor.matmul_mx(
-                    out=last[kt][:],
-                    lhsT=words[:, E - 1, 2 * kt * P : 2 * (kt + 1) * P].bitcast(FP4X4),
-                    lhsT_scale=plane[:, E - 1, kt * P : (kt + 1) * P],
-                    rhs=codes[E - 1][:, G - 1, w, :].bitcast(FP8X4),
-                    rhs_scale=scales[E - 1][:, G - 1, w, :],
-                    start=(w == 1), stop=(w == 0),
-                )
+                second_pass(last_banks[kt][:, 0, :], last, kt, w, w == 1, w == 0)
         for kt in range(KT):
-            nc.scalar.copy(dx[kt][:, S - P : S], last[kt][:])
+            nc.scalar.copy(dx[kt][:, S - P : S], last_banks[kt][:, 0, :])
 
         first = [keep.tile([P, T], F32, name="first_%d" % kt) for kt in range(KT)]
         total = [keep.tile([P, T], F32, name="total_%d" % kt) for kt in range(KT)]

@@ -9,8 +9,8 @@ P = 128
 PACK = 4
 G = C // P
 KT = K // P
-TURN_BANKS = 4
-RUN = 4
+TURN_BANKS = 5
+RUN = 2
 
 FLOPS = 2 * S * (N * H + 2 * H * K)
 BYTES = 4 * (2 * H * S + S + K * T) + (N * T + N * T // 32) + E * (N * H + 2 * H * K) * 17 // 32 + 2 * P * (S + 2 * T) // 16
@@ -38,7 +38,7 @@ def tile_moe_bdx_glu_silu_kernel(
         psum = ctx.enter_context(tc.psum_pool(name="psum", bufs=1))
         sum_banks = [psum.tile([P, H], F32, name="sum_bank_%d" % b) for b in range(2)]
         turn_banks = [psum.tile([P, PACK, P], F32, name="turn_bank_%d" % b) for b in range(TURN_BANKS)]
-        dx_banks = [psum.tile([P, PACK, P], F32, name="dx_bank_%d" % b) for b in range(2)]
+        dx_banks = [psum.tile([P, PACK, P], F32, name="dx_bank"), turn_banks[2]]
 
         offs_sb = keep.tile([P, S // 16], U16, name="offs_sb")
         pos1_sb = keep.tile([P, T // 16], U16, name="pos1_sb")
@@ -93,12 +93,12 @@ def tile_moe_bdx_glu_silu_kernel(
         load_saved(a1_sb, a1, "a1", 1, 2)
         load_words(w2_w, w2_words, 0, 2)
         load_scales(w2_s, w2_scales)
-        load_saved(a3_sb, a3, "a3", 0, 1)
-        for e in range(2, E):
-            load_saved(a1_sb, a1, "a1", e, e + 1)
-            if e % 2 == 0:
-                load_words(w2_w, w2_words, e, e + 2)
-            load_saved(a3_sb, a3, "a3", e - 1, e)
+        for e in range(E - 1):
+            if e + 2 < E:
+                load_saved(a1_sb, a1, "a1", e + 2, e + 3)
+            load_saved(a3_sb, a3, "a3", e, e + 1)
+            if e % 2 == 1:
+                load_words(w2_w, w2_words, e + 1, e + 3)
         load_scales(w1_s, w1_scales)
         load_saved(a3_sb, a3, "a3", E - 1, E)
         load_scales(w3_s, w3_scales)
@@ -134,14 +134,14 @@ def tile_moe_bdx_glu_silu_kernel(
             nc.scalar.activation(neg[e][:], a1_sb[e].rearrange("p t (g j) -> p g t j", j=P), ACT.Silu, scale=-1.0)
             if e == E - 1:
                 nc.scalar.activation(rest_last[:], neg[e][:], ACT.Identity, bias=1.0, scale=-1.0)
-            elif e >= 2:
+            elif e >= 1:
                 nc.scalar.activation(neg[e][:, 1, :, :], neg[e][:, 1, :, :], ACT.Identity, bias=1.0, scale=-1.0)
 
         def make_y(n):
             e, g = divmod(n, G)
             y_sb[n] = sig[:, n, :, :] if e >= 2 else keep.tile([P, PACK, P], F32, name="y_%d" % n)[:]
             factor = (neg[e] if e < E - 1 else rest_last)[:, g, :, :]
-            if e < 2 or (g == 0 and e < E - 1):
+            if e == 0 or (g == 0 and e < E - 1):
                 nc.gpsimd.tensor_scalar(y_sb[n], factor, -1.0, 1.0, ALU.mult, ALU.add)
                 factor = y_sb[n]
             nc.gpsimd.tensor_tensor(y_sb[n], factor, by_group(a3_sb, n), ALU.mult)

@@ -38,7 +38,7 @@ def tile_moe_bdx_glu_silu_kernel(
         psum = ctx.enter_context(tc.psum_pool(name="psum", bufs=1))
         sum_banks = [psum.tile([P, H], F32, name="sum_bank_%d" % b) for b in range(2)]
         turn_banks = [psum.tile([P, PACK, P], F32, name="turn_bank_%d" % b) for b in range(TURN_BANKS)]
-        dx_banks = [psum.tile([P, PACK, P], F32, name="dx_bank"), turn_banks[2]]
+        dx_bank = psum.tile([P, PACK, P], F32, name="dx_bank")
 
         offs_sb = keep.tile([P, S // 16], U16, name="offs_sb")
         pos1_sb = keep.tile([P, T // 16], U16, name="pos1_sb")
@@ -109,8 +109,8 @@ def tile_moe_bdx_glu_silu_kernel(
 
         blocks = S // PACK // P
         for b in range(blocks):
-            nc.tensor.transpose(dx_banks[0][:, b, :], gate_rows[:, b * P : (b + 1) * P], ident[:])
-        nc.scalar.copy(gate_col[:].rearrange("p (r b) -> p r b", b=blocks), dx_banks[0][:, 0:blocks, 0:PACK].rearrange("p b r -> p r b"))
+            nc.tensor.transpose(dx_bank[:, b, :], gate_rows[:, b * P : (b + 1) * P], ident[:])
+        nc.scalar.copy(gate_col[:].rearrange("p (r b) -> p r b", b=blocks), dx_bank[:, 0:blocks, 0:PACK].rearrange("p b r -> p r b"))
 
         def gather_words(j0, j1):
             nc.vector.tensor_copy(g_w[:, j0 % (S - C) : j0 % (S - C) + j1 - j0], dy_w[:].bitcast(U32).indirect(offs_sb[:, j0 // 16 : j1 // 16]))
@@ -124,7 +124,7 @@ def tile_moe_bdx_glu_silu_kernel(
         th.append(keep.tile([P, G, PACK, P], F32, name="th_last", tag="dx_1"))
         neg = [keep.tile([P, G, PACK, P], F32, name="neg_0")] + th[1 : E - 1]
         neg.append(keep.tile([P, G, PACK, P], F32, name="neg_last", tag="dx_0"))
-        rest_last = keep.tile([P, G, PACK, P], F32, name="rest_last")
+        rest_last = keep.tile([P, G, PACK, P], F32, name="rest_last", tag="codes_%d" % (E - 2), align_bytes=64)
         dx = []
 
         def by_group(saved, n):
@@ -133,15 +133,16 @@ def tile_moe_bdx_glu_silu_kernel(
         def make_neg(e):
             nc.scalar.activation(neg[e][:], a1_sb[e].rearrange("p t (g j) -> p g t j", j=P), ACT.Silu, scale=-1.0)
             if e == E - 1:
-                nc.scalar.activation(rest_last[:], neg[e][:], ACT.Identity, bias=1.0, scale=-1.0)
-            elif e >= 1:
+                for g in range(G):
+                    nc.scalar.activation(rest_last[:, g, :, :], neg[e][:, g, :, :], ACT.Identity, bias=1.0, scale=-1.0)
+            elif e >= 2:
                 nc.scalar.activation(neg[e][:, 1, :, :], neg[e][:, 1, :, :], ACT.Identity, bias=1.0, scale=-1.0)
 
         def make_y(n):
             e, g = divmod(n, G)
-            y_sb[n] = sig[:, n, :, :] if e >= 2 else keep.tile([P, PACK, P], F32, name="y_%d" % n)[:]
+            y_sb[n] = sig[:, n, :, :] if 2 * G <= n < E * G - 1 else keep.tile([P, PACK, P], F32, name="y_%d" % n)[:]
             factor = (neg[e] if e < E - 1 else rest_last)[:, g, :, :]
-            if e == 0 or (g == 0 and e < E - 1):
+            if e < 2 or (g == 0 and e < E - 1):
                 nc.gpsimd.tensor_scalar(y_sb[n], factor, -1.0, 1.0, ALU.mult, ALU.add)
                 factor = y_sb[n]
             nc.gpsimd.tensor_tensor(y_sb[n], factor, by_group(a3_sb, n), ALU.mult)
@@ -155,7 +156,7 @@ def tile_moe_bdx_glu_silu_kernel(
             nc.scalar.activation(sig[:, e * G : (e + 1) * G, :, :], th[e][:], ACT.Identity, bias=0.5, scale=0.5)
 
         def turned(n):
-            return turn_banks[(n + 2) % TURN_BANKS] if n < 10 else dx_banks[n - 10]
+            return turn_banks[(n + 2) % TURN_BANKS] if n < 11 else dx_bank
 
         def first_product(n):
             e = n // G
@@ -176,9 +177,12 @@ def tile_moe_bdx_glu_silu_kernel(
         def make_da(n, w):
             e, g = divmod(n, G)
             if (g, w) == (0, 1):
-                da_sb[e] = keep.tile([P, G, 2, P * PACK], BF16, name="da_%d" % e, align_bytes=64)
-                codes[e] = keep.tile([P, G, 2, P], U32, name="codes_%d" % e, align_bytes=64)
-                scales[e] = keep.tile([P, G, 2, P], U8, name="scales_%d" % e, align_bytes=64)
+                da_sb[e] = keep.tile([P, G, 2, P * PACK], BF16, name="da_%d" % e, tag="da_%d" % e, align_bytes=64)
+            if (n, w) == (E * G - 1, 1):
+                da_sb[E] = keep.tile([P, G, 2, P * PACK], BF16, name="da_last", tag="da_%d" % (E - 2), align_bytes=64)
+                e = E
+            if n == E * G - 1:
+                e = E
             factor = (y_sb[n], by_group(a1_sb, n))[w]
             nc.vector.tensor_tensor(
                 da_sb[e][:, g, w, :].rearrange("p (c i t) -> p c t i", i=RUN, t=PACK),
@@ -187,8 +191,14 @@ def tile_moe_bdx_glu_silu_kernel(
                 ALU.mult,
             )
 
-        def quantize(e, pick):
-            nc.vector.quantize_mx(out=pick(codes[e]).bitcast(FP8X4), scales=pick(scales[e]), in_=pick(da_sb[e]))
+        def quantize(e, pick, source):
+            if e not in codes:
+                codes[e] = keep.tile([P, G, 2, P], U32, name="codes_%d" % e, tag="codes_%d" % e, align_bytes=64)
+                scales[e] = keep.tile([P, G, 2, P], U8, name="scales_%d" % e, align_bytes=64)
+            nc.vector.quantize_mx(out=pick(codes[e]).bitcast(FP8X4), scales=pick(scales[e]), in_=pick(da_sb[source]))
+
+        def whole(tile):
+            return tile[:].rearrange("p g w j -> p (g w j)")
 
         def second_pass(out_cols, n, kt, w, start, stop):
             e, g = divmod(n, G)
@@ -238,19 +248,21 @@ def tile_moe_bdx_glu_silu_kernel(
                 make_neg(e + 2)
             if n + 2 <= last:
                 first_product(n + 2)
-            if g == 0 and e > 0:
-                quantize(e - 1, lambda tile: tile[:].rearrange("p g w j -> p (g w j)"))
+            if g == 0 and 0 < e < E - 1:
+                quantize(e - 1, whole, e - 1)
             if 4 <= n + 2 <= last:
                 make_y(n + 2)
             if n == last:
-                quantize(e, lambda tile: tile[:, 0, :, :].rearrange("p w j -> p (w j)"))
-                second_product(n - 1, n, turned(8))
+                quantize(e, lambda tile: tile[:, 0, :, :].rearrange("p w j -> p (w j)"), e)
+                second_product(n - 1, n, turned(7))
             make_da(n, 0)
+            if n == last - 1:
+                quantize(e - 1, whole, e - 1)
             if 6 <= n < last:
-                second_product((n - 6) * G, (n - 5) * G, (dx_banks + [turned(6), turned(7), turned(10)])[n - 6])
-        last_banks = (turned(9), turned(6))
+                second_product((n - 6) * G, (n - 5) * G, (dx_bank, turned(6), turned(7), turned(8), turned(6))[n - 6])
+        last_banks = (turned(9), turned(10))
         for w in (1, 0):
-            quantize(E - 1, lambda tile: tile[:, G - 1, w, :])
+            quantize(E - 1, lambda tile: tile[:, G - 1, w, :], E)
             for kt in range(KT):
                 second_pass(last_banks[kt][:, 0, :], last, kt, w, w == 1, w == 0)
         for kt in range(KT):

@@ -9,7 +9,7 @@ P = 128
 PACK = 4
 G = C // P
 KT = K // P
-TURN_BANKS = 5
+GROUP_BANKS = 4
 RUN = 2
 
 FLOPS = 2 * S * (N * H + 2 * H * K)
@@ -36,9 +36,8 @@ def tile_moe_bdx_glu_silu_kernel(
         keep = ctx.enter_context(tc.tile_pool(name="keep", bufs=1))
         ring = ctx.enter_context(tc.tile_pool(name="ring", bufs=3))
         psum = ctx.enter_context(tc.psum_pool(name="psum", bufs=1))
-        sum_banks = [psum.tile([P, H], F32, name="sum_bank_%d" % b) for b in range(2)]
-        turn_banks = [psum.tile([P, PACK, P], F32, name="turn_bank_%d" % b) for b in range(TURN_BANKS)]
-        dx_bank = psum.tile([P, PACK, P], F32, name="dx_bank")
+        group_banks = [psum.tile([P, PACK, P], F32, name="group_bank_%d" % b) for b in range(GROUP_BANKS)]
+        side_banks = [psum.tile([P, PACK, P], F32, name="side_bank_%d" % b) for b in range(4)]
 
         offs_sb = keep.tile([P, S // 16], U16, name="offs_sb")
         pos1_sb = keep.tile([P, T // 16], U16, name="pos1_sb")
@@ -92,25 +91,30 @@ def tile_moe_bdx_glu_silu_kernel(
         nc.sync.dma_start(out=dy_w[:], in_=dy_words[0].rearrange("p t d -> p (t d)").bitcast(I32))
         load_saved(a1_sb, a1, "a1", 1, 2)
         load_words(w2_w, w2_words, 0, 2)
+        load_saved(a3_sb, a3, "a3", 0, 1)
         load_scales(w2_s, w2_scales)
-        for e in range(E - 1):
-            if e + 2 < E:
-                load_saved(a1_sb, a1, "a1", e + 2, e + 3)
-            load_saved(a3_sb, a3, "a3", e, e + 1)
-            if e % 2 == 1:
-                load_words(w2_w, w2_words, e + 1, e + 3)
-        load_scales(w1_s, w1_scales)
+        load_saved(a1_sb, a1, "a1", 2, 3)
+        load_saved(a3_sb, a3, "a3", 1, 2)
+        load_saved(a1_sb, a1, "a1", E - 1, E)
+        load_saved(a1_sb, a1, "a1", 3, 4)
         load_saved(a3_sb, a3, "a3", E - 1, E)
+        load_saved(a1_sb, a1, "a1", 4, 5)
+        load_words(w2_w, w2_words, 2, 4)
+        load_saved(a3_sb, a3, "a3", 2, 3)
+        load_words(w2_w, w2_words, 4, E)
+        load_saved(a3_sb, a3, "a3", 3, 4)
+        load_saved(a3_sb, a3, "a3", 4, 5)
+        load_scales(w1_s, w1_scales)
         load_scales(w3_s, w3_scales)
-        load_words(w1_w, w1_words, 0, E)
         load_words(w3_w, w3_words, 0, E)
+        load_words(w1_w, w1_words, 0, E)
         nc.sync.dma_start(pos1_sb[:], pos1)
         nc.sync.dma_start(pos2_sb[:], pos2)
 
         blocks = S // PACK // P
         for b in range(blocks):
-            nc.tensor.transpose(dx_bank[:, b, :], gate_rows[:, b * P : (b + 1) * P], ident[:])
-        nc.scalar.copy(gate_col[:].rearrange("p (r b) -> p r b", b=blocks), dx_bank[:, 0:blocks, 0:PACK].rearrange("p b r -> p r b"))
+            nc.tensor.transpose(side_banks[3][:, b, :], gate_rows[:, b * P : (b + 1) * P], ident[:])
+        nc.scalar.copy(gate_col[:].rearrange("p (r b) -> p r b", b=blocks), side_banks[3][:, 0:blocks, 0:PACK].rearrange("p b r -> p r b"))
 
         def gather_words(j0, j1):
             nc.vector.tensor_copy(g_w[:, j0 % (S - C) : j0 % (S - C) + j1 - j0], dy_w[:].bitcast(U32).indirect(offs_sb[:, j0 // 16 : j1 // 16]))
@@ -118,103 +122,107 @@ def tile_moe_bdx_glu_silu_kernel(
         def gather_bytes(j0, j1):
             nc.vector.tensor_copy(g_s[:, j0 % (S - C) : j0 % (S - C) + j1 - j0], dy_s[:].indirect(offs_sb[:, j0 // 16 : j1 // 16]))
 
-        y_sb, da_sb, codes, scales = {}, {}, {}, {}
+        y_sb, da_sb, codes, scales, th, rest = {}, {}, {}, {}, {}, {}
         sig = keep.tile([P, E * G, PACK, P], F32, name="sig")
-        th = [keep.tile([P, G, PACK, P], F32, name="th_%d" % e) for e in range(E - 1)]
-        th.append(keep.tile([P, G, PACK, P], F32, name="th_last", tag="dx_1"))
-        neg = [keep.tile([P, G, PACK, P], F32, name="neg_0")] + th[1 : E - 1]
-        neg.append(keep.tile([P, G, PACK, P], F32, name="neg_last", tag="dx_0"))
-        rest_last = keep.tile([P, G, PACK, P], F32, name="rest_last", tag="codes_%d" % (E - 2), align_bytes=64)
         dx = []
+        last = E * G - 1
 
         def by_group(saved, n):
             return saved[n // G][:, :, n % G * P : (n % G + 1) * P]
 
-        def make_neg(e):
-            nc.scalar.activation(neg[e][:], a1_sb[e].rearrange("p t (g j) -> p g t j", j=P), ACT.Silu, scale=-1.0)
-            if e == E - 1:
-                for g in range(G):
-                    nc.scalar.activation(rest_last[:, g, :, :], neg[e][:, g, :, :], ACT.Identity, bias=1.0, scale=-1.0)
-            elif e >= 2:
-                nc.scalar.activation(neg[e][:, 1, :, :], neg[e][:, 1, :, :], ACT.Identity, bias=1.0, scale=-1.0)
+        def make_silu(e):
+            rest[e] = keep.tile([P, PACK, C], F32, name="rest_%d" % e, tag="chain_%d" % {1: E, E - 1: 1}.get(e, e), align_bytes=64)
+            nc.scalar.activation(rest[e][:], a1_sb[e], ACT.Silu, scale=-1.0)
 
-        def make_y(n):
-            e, g = divmod(n, G)
-            y_sb[n] = sig[:, n, :, :] if 2 * G <= n < E * G - 1 else keep.tile([P, PACK, P], F32, name="y_%d" % n)[:]
-            factor = (neg[e] if e < E - 1 else rest_last)[:, g, :, :]
-            if e < 2 or (g == 0 and e < E - 1):
-                nc.gpsimd.tensor_scalar(y_sb[n], factor, -1.0, 1.0, ALU.mult, ALU.add)
-                factor = y_sb[n]
-            nc.gpsimd.tensor_tensor(y_sb[n], factor, by_group(a3_sb, n), ALU.mult)
+        def make_rest(e):
+            nc.scalar.activation(rest[e][:], rest[e][:], ACT.Identity, bias=1.0, scale=-1.0)
 
-        def make_sigmoid(e):
-            for g in range(G):
-                a1_t = turn_banks[(e * G + g) % TURN_BANKS]
-                for t in range(PACK):
-                    nc.tensor.transpose(a1_t[:, t, :], by_group(a1_sb, e * G + g)[:, t, :], ident[:])
-                nc.scalar.activation(th[e][:, g, :, :], a1_t[:], ACT.Tanh, scale=0.5)
-            nc.scalar.activation(sig[:, e * G : (e + 1) * G, :, :], th[e][:], ACT.Identity, bias=0.5, scale=0.5)
+        def rest_on_gpsimd(e, tag):
+            neg = rest[e]
+            rest[e] = keep.tile([P, PACK, C], F32, name="rest_apart_%d" % e, tag=tag, align_bytes=64)
+            nc.gpsimd.tensor_scalar(rest[e][:], neg[:], -1.0, 1.0, ALU.mult, ALU.add)
+
+        def make_y(e, tag, parts):
+            y_sb[e] = keep.tile([P, PACK, C], F32, name="y_%d" % e, tag=tag, align_bytes=64)
+            for j in range(0, C, C // parts):
+                cols = slice(j, j + C // parts)
+                nc.gpsimd.tensor_tensor(y_sb[e][:, :, cols], rest[e][:, :, cols], a3_sb[e][:, :, cols], ALU.mult)
+
+        def make_tanh(n):
+            tag = "dx_%d" % (n % G) if n >= last - 1 else "chain_%d" % (n // G) if n % G == 0 and n > 0 else "th_%d" % n
+            th[n] = keep.tile([P, PACK, P], F32, name="th_%d" % n, tag=tag, align_bytes=64)
+            a1_t = side_banks[n % 4]
+            for t in range(PACK):
+                nc.tensor.transpose(a1_t[:, t, :], by_group(a1_sb, n)[:, t, :], ident[:])
+            nc.scalar.activation(th[n][:], a1_t[:], ACT.Tanh, scale=0.5)
+
+        def make_sigmoid(n):
+            nc.scalar.activation(sig[:, n, :, :], th[n][:], ACT.Identity, bias=0.5, scale=0.5)
 
         def turned(n):
-            return turn_banks[(n + 2) % TURN_BANKS] if n < 11 else dx_bank
+            return group_banks[n % GROUP_BANKS] if n < last - 1 else side_banks[n % G]
 
         def first_product(n):
             e = n // G
             cols = slice(n * P % (S - C), n * P % (S - C) + P)
-            acc = sum_banks[n % 2]
+            bank = group_banks[n % GROUP_BANKS]
+            acc = bank[:].rearrange("j t p -> j (t p)")
             nc.tensor.matmul_mx(
-                out=acc[:], lhsT=g_w[:, cols].bitcast(FP8X4), lhsT_scale=g_s[:, cols],
+                out=acc, lhsT=g_w[:, cols].bitcast(FP8X4), lhsT_scale=g_s[:, cols],
                 rhs=w2_w[:, e, :].bitcast(FP4X4), rhs_scale=w2_s[:, e, :], start=True, stop=True,
             )
-            m = ring.tile([P, PACK, P], F32, name="m")[:] if n < 3 else y_sb[n - 3]
+            m = ring.tile([P, PACK, P], F32, name="m")
             nc.vector.scalar_tensor_tensor(
-                m, acc[:].rearrange("j (p t) -> j t p", t=PACK), gate_col[:, n : n + 1], sig[:, n, :, :],
+                m[:], acc.rearrange("j (p t) -> j t p", t=PACK), gate_col[:, n : n + 1], sig[:, n, :, :],
                 ALU.mult, ALU.mult,
             )
             for t in range(PACK):
                 nc.tensor.transpose(turned(n)[:, t, :], m[:, t, :], ident[:])
 
+        def codes_tag(j):
+            return ("apart_held", "apart_1", "chain_2", "chain_3", "chain_4", "codes_5", "codes_6")[j]
+
+        def place(n, w):
+            return divmod(2 * n + 2 - w, 4)
+
         def make_da(n, w):
-            e, g = divmod(n, G)
-            if (g, w) == (0, 1):
-                da_sb[e] = keep.tile([P, G, 2, P * PACK], BF16, name="da_%d" % e, tag="da_%d" % e, align_bytes=64)
-            if (n, w) == (E * G - 1, 1):
-                da_sb[E] = keep.tile([P, G, 2, P * PACK], BF16, name="da_last", tag="da_%d" % (E - 2), align_bytes=64)
-                e = E
-            if n == E * G - 1:
-                e = E
-            factor = (y_sb[n], by_group(a1_sb, n))[w]
+            j, k = place(n, w)
+            if j not in da_sb:
+                da_sb[j] = keep.tile([P, 4, P * PACK], BF16, name="da_%d" % j, tag="slot_%d" % (j % 3), align_bytes=64)
+            factor = by_group((y_sb, a1_sb)[w], n)
             nc.vector.tensor_tensor(
-                da_sb[e][:, g, w, :].rearrange("p (c i t) -> p c t i", i=RUN, t=PACK),
+                da_sb[j][:, k, :].rearrange("p (c i t) -> p c t i", i=RUN, t=PACK),
                 turned(n)[:].rearrange("p t (c i) -> p c t i", i=RUN),
                 factor.rearrange("p t (c i) -> p c t i", i=RUN),
                 ALU.mult,
             )
 
-        def quantize(e, pick, source):
-            if e not in codes:
-                codes[e] = keep.tile([P, G, 2, P], U32, name="codes_%d" % e, tag="codes_%d" % e, align_bytes=64)
-                scales[e] = keep.tile([P, G, 2, P], U8, name="scales_%d" % e, align_bytes=64)
-            nc.vector.quantize_mx(out=pick(codes[e]).bitcast(FP8X4), scales=pick(scales[e]), in_=pick(da_sb[source]))
-
-        def whole(tile):
-            return tile[:].rearrange("p g w j -> p (g w j)")
+        def quantize(j, k0, k1):
+            if j not in codes:
+                codes[j] = keep.tile([P, 4, P], U32, name="codes_%d" % j, tag=codes_tag(j), align_bytes=64)
+                scales[j] = keep.tile([P, 4, P], U8, name="scales_%d" % j, align_bytes=64)
+            nc.vector.quantize_mx(
+                out=codes[j][:, k0:k1, :].rearrange("p k j -> p (k j)").bitcast(FP8X4),
+                scales=scales[j][:, k0:k1, :].rearrange("p k j -> p (k j)"),
+                in_=da_sb[j][:, k0:k1, :].rearrange("p k j -> p (k j)"),
+            )
 
         def second_pass(out_cols, n, kt, w, start, stop):
-            e, g = divmod(n, G)
+            e = n // G
+            j, k = place(n, w)
             words, plane = ((w1_w, w1_s), (w3_w, w3_s))[w]
             nc.tensor.matmul_mx(
                 out=out_cols,
                 lhsT=words[:, e, 2 * kt * P : 2 * (kt + 1) * P].bitcast(FP4X4),
                 lhsT_scale=plane[:, e, kt * P : (kt + 1) * P],
-                rhs=codes[e][:, g, w, :].bitcast(FP8X4),
-                rhs_scale=scales[e][:, g, w, :],
+                rhs=codes[j][:, k, :].bitcast(FP8X4),
+                rhs_scale=scales[j][:, k, :],
                 start=start, stop=stop,
             )
 
         def second_product(n0, n1, bank):
             if not dx:
-                dx.extend(keep.tile([P, S], F32, name="dx_%d" % kt, tag="dx_%d" % kt) for kt in range(KT))
+                dx.extend(keep.tile([P, S], F32, name="dx_%d" % kt, tag="dx_%d" % kt, align_bytes=64) for kt in range(KT))
             for kt in range(KT):
                 for n in range(n0, n1):
                     for w in range(2):
@@ -227,42 +235,62 @@ def tile_moe_bdx_glu_silu_kernel(
         for gather in (gather_bytes, gather_words):
             for j0, j1 in ((0, 2 * C), (2 * C, 4 * C), (4 * C, 5 * C)):
                 gather(j0, j1)
-        make_neg(0)
-        make_y(0)
-        make_y(1)
-        make_sigmoid(0)
-        make_sigmoid(1)
-        make_neg(1)
-        make_y(2)
-        make_y(3)
+        make_silu(0)
+        rest_on_gpsimd(0, "apart_0")
+        make_y(0, "y_first", G)
+        for e in range(2):
+            for step in (make_tanh, make_sigmoid):
+                for g in range(G):
+                    step(e * G + g)
+            early = (1, E - 1)[e]
+            make_silu(early)
+            rest_on_gpsimd(early, ("apart_1", "apart_held")[e])
+            make_y(early, ("y_second", "y_held")[e], 1)
         first_product(0)
         first_product(1)
         gather_words(S - C, S)
         gather_bytes(S - C, S)
-        last = E * G - 1
-        for n in range(E * G):
-            e, g = divmod(n, G)
+        for e in range(E - 1):
+            n = e * G
+            if e + 2 < E:
+                make_tanh(n + 4)
+                if e > 0:
+                    make_rest(e + 1)
+                make_tanh(n + 5)
+                make_sigmoid(n + 4)
+                make_sigmoid(n + 5)
+                if e + 3 < E:
+                    make_silu(e + 2)
+            if e == E - 2:
+                for b, (n0, n1) in enumerate(((0, 1), (1, 3), (3, 5))):
+                    second_product(n0, n1, side_banks[b])
             make_da(n, 1)
-            if g == 0 and e + 2 < E:
-                make_sigmoid(e + 2)
-                make_neg(e + 2)
-            if n + 2 <= last:
-                first_product(n + 2)
-            if g == 0 and 0 < e < E - 1:
-                quantize(e - 1, whole, e - 1)
-            if 4 <= n + 2 <= last:
-                make_y(n + 2)
-            if n == last:
-                quantize(e, lambda tile: tile[:, 0, :, :].rearrange("p w j -> p (w j)"), e)
-                second_product(n - 1, n, turned(7))
+            make_da(n + 1, 1)
+            first_product(n + 2)
             make_da(n, 0)
-            if n == last - 1:
-                quantize(e - 1, whole, e - 1)
-            if 6 <= n < last:
-                second_product((n - 6) * G, (n - 5) * G, (dx_bank, turned(6), turned(7), turned(8), turned(6))[n - 6])
-        last_banks = (turned(9), turned(10))
+            first_product(n + 3)
+            make_da(n + 1, 0)
+            if e == 1:
+                quantize(0, 1, 2)
+                quantize(0, 2, 4)
+            if e > 0:
+                quantize(e, 0, 4)
+            if 0 < e < E - 2:
+                make_y(e + 1, "slot_%d" % (e % 3), G)
+        second_product(5, 7, side_banks[3])
+        second_product(7, 9, group_banks[2])
+        make_da(last - 1, 1)
+        make_da(last - 1, 0)
+        quantize(E - 1, 0, 2)
+        second_product(9, 10, group_banks[3])
+        make_da(last, 1)
+        quantize(E - 1, 2, 3)
+        second_product(10, 11, side_banks[2])
+        make_da(last, 0)
+        last_banks = group_banks[0:KT]
         for w in (1, 0):
-            quantize(E - 1, lambda tile: tile[:, G - 1, w, :], E)
+            j, k = place(last, w)
+            quantize(j, k, k + 1)
             for kt in range(KT):
                 second_pass(last_banks[kt][:, 0, :], last, kt, w, w == 1, w == 0)
         for kt in range(KT):

@@ -11,6 +11,7 @@ G = C // P
 KT = K // P
 GROUP_BANKS = 4
 RUN = 2
+OFF_VECTOR = (2, 3)
 
 FLOPS = 2 * S * (N * H + 2 * H * K)
 BYTES = 4 * (2 * H * S + S + K * T) + (N * T + N * T // 32) + E * (N * H + 2 * H * K) * 17 // 32 + 2 * P * (S + 2 * T) // 16
@@ -45,7 +46,7 @@ def tile_moe_bdx_glu_silu_kernel(
         dy_w = keep.tile([P, T], I32, name="dy_w", align_bytes=64)
         dy_s = keep.tile([P, T], U8, name="dy_s", align_bytes=64)
         g_w = keep.tile([P, S - C], U32, name="g_w", align_bytes=64)
-        g_s = keep.tile([P, S - C], U8, name="g_s", align_bytes=64)
+        g_s = keep.tile([P, S], U8, name="g_s", align_bytes=64)
         w2_w = keep.tile([P, E, 2 * H], U8, name="w2_w", align_bytes=64)
         w1_w = keep.tile([P, E, 2 * K], U8, name="w1_w", align_bytes=64)
         w3_w = keep.tile([P, E, 2 * K], U8, name="w3_w", align_bytes=64)
@@ -77,52 +78,46 @@ def tile_moe_bdx_glu_silu_kernel(
                 in_=src[e0:e1, 0, :, :].rearrange("e p b -> p e b").bitcast(I32),
             )
 
-        def load_saved(views, src, name, e0, e1):
+        def load_saved(views, src, name, e0, e1, queue=nc.sync):
             tile = keep.tile([P, PACK, (e1 - e0) * C], F32, name="%s_%d" % (name, e0))
-            nc.sync.dma_start(out=tile[:], in_=src[:, e0 * C : e1 * C].rearrange("(p t) c -> p t c", t=PACK))
+            queue.dma_start(out=tile[:], in_=src[:, e0 * C : e1 * C].rearrange("(p t) c -> p t c", t=PACK))
             for e in range(e0, e1):
                 views[e] = tile[:, :, (e - e0) * C : (e - e0 + 1) * C]
 
         nc.sync.dma_start(offs_sb[:], offs)
         for r in range(4):
             nc.sync.dma_start(out=dy_s[r:P:32, :].bitcast(I32), in_=dy_scales[0, r:16:4, :].bitcast(I32))
-        nc.sync.dma_start(out=gate_rows[0:PACK, :], in_=gate[0, :].rearrange("(r c) -> r c", r=PACK))
-        load_saved(a1_sb, a1, "a1", 0, 1)
+        load_saved(a1_sb, a1, "a1", 0, 1, nc.scalar)
         nc.sync.dma_start(out=dy_w[:], in_=dy_words[0].rearrange("p t d -> p (t d)").bitcast(I32))
         load_saved(a1_sb, a1, "a1", 1, 2)
+        nc.sync.dma_start(out=gate_rows[0:PACK, :], in_=gate[0, :].rearrange("(r c) -> r c", r=PACK))
+        nc.sync.dma_start(pos1_sb[:], pos1)
+        nc.sync.dma_start(pos2_sb[:], pos2)
         load_words(w2_w, w2_words, 0, 2)
         load_saved(a3_sb, a3, "a3", 0, 1)
         load_scales(w2_s, w2_scales)
         load_saved(a1_sb, a1, "a1", 2, 3)
         load_saved(a3_sb, a3, "a3", 1, 2)
-        load_saved(a1_sb, a1, "a1", E - 1, E)
         load_saved(a1_sb, a1, "a1", 3, 4)
-        load_saved(a3_sb, a3, "a3", E - 1, E)
-        load_saved(a1_sb, a1, "a1", 4, 5)
         load_words(w2_w, w2_words, 2, 4)
+        load_saved(a1_sb, a1, "a1", 4, 5)
         load_saved(a3_sb, a3, "a3", 2, 3)
         load_words(w2_w, w2_words, 4, E)
-        load_saved(a3_sb, a3, "a3", 3, 4)
-        load_saved(a3_sb, a3, "a3", 4, 5)
+        load_saved(a1_sb, a1, "a1", 5, 6)
+        for e in range(3, E):
+            load_saved(a3_sb, a3, "a3", e, e + 1)
         load_scales(w1_s, w1_scales)
         load_scales(w3_s, w3_scales)
         load_words(w3_w, w3_words, 0, E)
         load_words(w1_w, w1_words, 0, E)
-        nc.sync.dma_start(pos1_sb[:], pos1)
-        nc.sync.dma_start(pos2_sb[:], pos2)
-
-        blocks = S // PACK // P
-        for b in range(blocks):
-            nc.tensor.transpose(side_banks[3][:, b, :], gate_rows[:, b * P : (b + 1) * P], ident[:])
-        nc.scalar.copy(gate_col[:].rearrange("p (r b) -> p r b", b=blocks), side_banks[3][:, 0:blocks, 0:PACK].rearrange("p b r -> p r b"))
 
         def gather_words(j0, j1):
             nc.vector.tensor_copy(g_w[:, j0 % (S - C) : j0 % (S - C) + j1 - j0], dy_w[:].bitcast(U32).indirect(offs_sb[:, j0 // 16 : j1 // 16]))
 
         def gather_bytes(j0, j1):
-            nc.vector.tensor_copy(g_s[:, j0 % (S - C) : j0 % (S - C) + j1 - j0], dy_s[:].indirect(offs_sb[:, j0 // 16 : j1 // 16]))
+            nc.vector.tensor_copy(g_s[:, j0:j1], dy_s[:].indirect(offs_sb[:, j0 // 16 : j1 // 16]))
 
-        y_sb, da_sb, codes, scales, th, rest = {}, {}, {}, {}, {}, {}
+        y_sb, da_sb, codes, scales, th, rest, apart, m_sb = {}, {}, {}, {}, {}, {}, {}, {}
         sig = keep.tile([P, E * G, PACK, P], F32, name="sig")
         dx = []
         last = E * G - 1
@@ -131,11 +126,15 @@ def tile_moe_bdx_glu_silu_kernel(
             return saved[n // G][:, :, n % G * P : (n % G + 1) * P]
 
         def make_silu(e):
-            rest[e] = keep.tile([P, PACK, C], F32, name="rest_%d" % e, tag="chain_%d" % {1: E, E - 1: 1}.get(e, e), align_bytes=64)
+            rest[e] = keep.tile([P, PACK, C], F32, name="rest_%d" % e, tag={1: "rest_1", E - 1: "dx_1"}.get(e, "chain_%d" % e), align_bytes=64)
             nc.scalar.activation(rest[e][:], a1_sb[e], ACT.Silu, scale=-1.0)
 
         def make_rest(e):
             nc.scalar.activation(rest[e][:], rest[e][:], ACT.Identity, bias=1.0, scale=-1.0)
+
+        def rest_apart(n):
+            apart[n] = keep.tile([P, PACK, P], F32, name="rest_group_%d" % n, tag="th_%d" % (2 * (n % G) + 1), align_bytes=64)
+            nc.scalar.activation(apart[n][:], by_group(rest, n), ACT.Identity, bias=1.0, scale=-1.0)
 
         def rest_on_gpsimd(e, tag):
             neg = rest[e]
@@ -149,7 +148,7 @@ def tile_moe_bdx_glu_silu_kernel(
                 nc.gpsimd.tensor_tensor(y_sb[e][:, :, cols], rest[e][:, :, cols], a3_sb[e][:, :, cols], ALU.mult)
 
         def make_tanh(n):
-            tag = "dx_%d" % (n % G) if n >= last - 1 else "chain_%d" % (n // G) if n % G == 0 and n > 0 else "th_%d" % n
+            tag = "dx_%d" % (1 - n % G) if n >= last - 1 else "chain_%d" % (n // G) if n % G == 0 and n > 0 else "th_%d" % n
             th[n] = keep.tile([P, PACK, P], F32, name="th_%d" % n, tag=tag, align_bytes=64)
             a1_t = side_banks[n % 4]
             for t in range(PACK):
@@ -162,25 +161,29 @@ def tile_moe_bdx_glu_silu_kernel(
         def turned(n):
             return group_banks[n % GROUP_BANKS] if n < last - 1 else side_banks[n % G]
 
-        def first_product(n):
+        def first_sums(n, bank):
             e = n // G
             cols = slice(n * P % (S - C), n * P % (S - C) + P)
-            bank = group_banks[n % GROUP_BANKS]
             acc = bank[:].rearrange("j t p -> j (t p)")
             nc.tensor.matmul_mx(
-                out=acc, lhsT=g_w[:, cols].bitcast(FP8X4), lhsT_scale=g_s[:, cols],
+                out=acc, lhsT=g_w[:, cols].bitcast(FP8X4), lhsT_scale=g_s[:, n * P : (n + 1) * P],
                 rhs=w2_w[:, e, :].bitcast(FP4X4), rhs_scale=w2_s[:, e, :], start=True, stop=True,
             )
-            m = ring.tile([P, PACK, P], F32, name="m")
-            nc.vector.scalar_tensor_tensor(
-                m[:], acc.rearrange("j (p t) -> j t p", t=PACK), gate_col[:, n : n + 1], sig[:, n, :, :],
-                ALU.mult, ALU.mult,
-            )
-            for t in range(PACK):
-                nc.tensor.transpose(turned(n)[:, t, :], m[:, t, :], ident[:])
+            return acc.rearrange("j (p t) -> j t p", t=PACK)
 
-        def codes_tag(j):
-            return ("apart_held", "apart_1", "chain_2", "chain_3", "chain_4", "codes_5", "codes_6")[j]
+        def gate_off_vector(n):
+            sums = first_sums(n, side_banks[n % 4])
+            m_sb[n] = keep.tile([P, PACK, P], F32, name="m_%d" % n)
+            nc.scalar.activation(m_sb[n][:], sums, ACT.Copy, scale=gate_col[:, n : n + 1])
+            nc.gpsimd.tensor_tensor(m_sb[n][:], m_sb[n][:], sig[:, n, :, :], ALU.mult)
+
+        def first_product(n):
+            if n not in OFF_VECTOR:
+                sums = first_sums(n, group_banks[n % GROUP_BANKS])
+                m_sb[n] = ring.tile([P, PACK, P], F32, name="m")
+                nc.vector.scalar_tensor_tensor(m_sb[n][:], sums, gate_col[:, n : n + 1], sig[:, n, :, :], ALU.mult, ALU.mult)
+            for t in range(PACK):
+                nc.tensor.transpose(turned(n)[:, t, :], m_sb[n][:, t, :], ident[:])
 
         def place(n, w):
             return divmod(2 * n + 2 - w, 4)
@@ -188,7 +191,7 @@ def tile_moe_bdx_glu_silu_kernel(
         def make_da(n, w):
             j, k = place(n, w)
             if j not in da_sb:
-                da_sb[j] = keep.tile([P, 4, P * PACK], BF16, name="da_%d" % j, tag="slot_%d" % (j % 3), align_bytes=64)
+                da_sb[j] = keep.tile([P, 4, P * PACK], BF16, name="da_%d" % j, tag="da_%d" % (j % 4), align_bytes=64)
             factor = by_group((y_sb, a1_sb)[w], n)
             nc.vector.tensor_tensor(
                 da_sb[j][:, k, :].rearrange("p (c i t) -> p c t i", i=RUN, t=PACK),
@@ -199,7 +202,7 @@ def tile_moe_bdx_glu_silu_kernel(
 
         def quantize(j, k0, k1):
             if j not in codes:
-                codes[j] = keep.tile([P, 4, P], U32, name="codes_%d" % j, tag=codes_tag(j), align_bytes=64)
+                codes[j] = keep.tile([P, 4, P], U32, name="codes_%d" % j, align_bytes=64)
                 scales[j] = keep.tile([P, 4, P], U8, name="scales_%d" % j, align_bytes=64)
             nc.vector.quantize_mx(
                 out=codes[j][:, k0:k1, :].rearrange("p k j -> p (k j)").bitcast(FP8X4),
@@ -232,35 +235,48 @@ def tile_moe_bdx_glu_silu_kernel(
                     dx[kt][:, n0 * P : n1 * P].rearrange("p (g j) -> p g j", j=P), bank[:, kt * G : kt * G + n1 - n0, :]
                 )
 
-        for gather in (gather_bytes, gather_words):
-            for j0, j1 in ((0, 2 * C), (2 * C, 4 * C), (4 * C, 5 * C)):
-                gather(j0, j1)
+        for j0 in range(0, S, 2 * C):
+            gather_bytes(j0, j0 + 2 * C)
+        for j0, j1 in ((0, 2 * C), (2 * C, 4 * C), (4 * C, 5 * C)):
+            gather_words(j0, j1)
         make_silu(0)
         rest_on_gpsimd(0, "apart_0")
-        make_y(0, "y_first", G)
+        make_y(0, "y_0", G)
         for e in range(2):
             for step in (make_tanh, make_sigmoid):
                 for g in range(G):
                     step(e * G + g)
-            early = (1, E - 1)[e]
-            make_silu(early)
-            rest_on_gpsimd(early, ("apart_1", "apart_held")[e])
-            make_y(early, ("y_second", "y_held")[e], 1)
+            if e == 0:
+                make_silu(1)
+                rest_on_gpsimd(1, "apart_1")
+                blocks = S // PACK // P
+                for b in range(blocks):
+                    nc.tensor.transpose(group_banks[3][:, b, :], gate_rows[:, b * P : (b + 1) * P], ident[:])
+                nc.scalar.copy(gate_col[:].rearrange("p (r b) -> p r b", b=blocks), group_banks[3][:, 0:blocks, 0:PACK].rearrange("p b r -> p r b"))
         first_product(0)
         first_product(1)
+        for n in OFF_VECTOR:
+            gate_off_vector(n)
+        make_y(1, "y_1", G)
         gather_words(S - C, S)
-        gather_bytes(S - C, S)
         for e in range(E - 1):
             n = e * G
             if e + 2 < E:
-                make_tanh(n + 4)
-                if e > 0:
-                    make_rest(e + 1)
-                make_tanh(n + 5)
-                make_sigmoid(n + 4)
-                make_sigmoid(n + 5)
-                if e + 3 < E:
-                    make_silu(e + 2)
+                for step in (make_tanh, make_sigmoid):
+                    for g in range(G):
+                        step(n + 4 + g)
+                make_silu(e + 2)
+                if e < 2:
+                    make_rest(e + 2)
+                    make_y(e + 2, "y_%d" % (e + 2), 1)
+                elif e == 2:
+                    rest_on_gpsimd(e + 2, "apart_4")
+                    make_y(e + 2, "y_4", G)
+                else:
+                    y_sb[E - 1] = keep.tile([P, PACK, C], F32, name="y_last")
+                    for k in (last - 1, last):
+                        rest_apart(k)
+                        nc.gpsimd.tensor_tensor(by_group(y_sb, k), apart[k][:], by_group(a3_sb, k), ALU.mult)
             if e == E - 2:
                 for b, (n0, n1) in enumerate(((0, 1), (1, 3), (3, 5))):
                     second_product(n0, n1, side_banks[b])
@@ -270,13 +286,11 @@ def tile_moe_bdx_glu_silu_kernel(
             make_da(n, 0)
             first_product(n + 3)
             make_da(n + 1, 0)
-            if e == 1:
+            if e == 0:
                 quantize(0, 1, 2)
                 quantize(0, 2, 4)
-            if e > 0:
+            else:
                 quantize(e, 0, 4)
-            if 0 < e < E - 2:
-                make_y(e + 1, "slot_%d" % (e % 3), G)
         second_product(5, 7, side_banks[3])
         second_product(7, 9, group_banks[2])
         make_da(last - 1, 1)
@@ -296,8 +310,8 @@ def tile_moe_bdx_glu_silu_kernel(
         for kt in range(KT):
             nc.scalar.copy(dx[kt][:, S - P : S], last_banks[kt][:, 0, :])
 
-        first = [keep.tile([P, T], F32, name="first_%d" % kt) for kt in range(KT)]
-        total = [keep.tile([P, T], F32, name="total_%d" % kt) for kt in range(KT)]
+        first = [keep.tile([P, T], F32, name="first_%d" % kt, tag="apart_%d" % kt, align_bytes=64) for kt in range(KT)]
+        total = [keep.tile([P, T], F32, name="total_%d" % kt, tag="y_%d" % kt, align_bytes=64) for kt in range(KT)]
         for kt in range(KT):
             nc.vector.tensor_copy(first[kt][:], dx[kt][:].indirect(pos1_sb[:]))
         for kt, t0, t1, queue in ((0, 0, T, nc.sync), (1, 0, 512, nc.sync), (1, 512, T, nc.scalar)):

@@ -61,9 +61,9 @@ def tile_moe_bdx_glu_silu_kernel(
         nc.gpsimd.memset(dy_s[:].bitcast(I32), 0)
         nc.gpsimd.memset(gate_rows[:], 0.0)
         make_identity(nc, ident[:])
-        nc.vector.memset(w2_s[:].bitcast(I32), 0)
-        nc.vector.memset(w1_s[:].bitcast(I32), 0)
-        nc.vector.memset(w3_s[:].bitcast(I32), 0)
+        nc.gpsimd.memset(w2_s[:].bitcast(I32), 0)
+        nc.gpsimd.memset(w1_s[:].bitcast(I32), 0)
+        nc.gpsimd.memset(w3_s[:].bitcast(I32), 0)
 
         def load_scales(plane, src):
             for r in range(4):

@@ -266,12 +266,9 @@ def tile_moe_bdx_glu_silu_kernel(
                     for g in range(G):
                         step(n + 4 + g)
                 make_silu(e + 2)
-                if e < 2:
+                if e < 3:
                     make_rest(e + 2)
-                    make_y(e + 2, "y_%d" % (e + 2), 1)
-                elif e == 2:
-                    rest_on_gpsimd(e + 2, "apart_4")
-                    make_y(e + 2, "y_4", G)
+                    make_y(e + 2, "y_%d" % (e + 2), 1 if e < 2 else G)
                 else:
                     y_sb[E - 1] = keep.tile([P, PACK, C], F32, name="y_last")
                     for k in (last - 1, last):

@@ -126,7 +126,7 @@ def tile_moe_bdx_glu_silu_kernel(
             return saved[n // G][:, :, n % G * P : (n % G + 1) * P]
 
         def make_silu(e):
-            rest[e] = keep.tile([P, PACK, C], F32, name="rest_%d" % e, tag={1: "rest_1", E - 1: "dx_1"}.get(e, "chain_%d" % e), align_bytes=64)
+            rest[e] = keep.tile([P, PACK, C], F32, name="rest_%d" % e, tag={1: "rest_1", 2: "rest_2", E - 1: "dx_1"}.get(e, "chain_%d" % e), align_bytes=64)
             nc.scalar.activation(rest[e][:], a1_sb[e], ACT.Silu, scale=-1.0)
 
         def make_rest(e):

@@ -12,6 +12,7 @@ KT = K // P
 GROUP_BANKS = 4
 RUN = 2
 OFF_VECTOR = (2, 3)
+VECTOR_FIRST = 192
 
 FLOPS = 2 * S * (N * H + 2 * H * K)
 BYTES = 4 * (2 * H * S + S + K * T) + (N * T + N * T // 32) + E * (N * H + 2 * H * K) * 17 // 32 + 2 * P * (S + 2 * T) // 16
@@ -304,15 +305,29 @@ def tile_moe_bdx_glu_silu_kernel(
             quantize(j, k, k + 1)
             for kt in range(KT):
                 second_pass(last_banks[kt][:, 0, :], last, kt, w, w == 1, w == 0)
-        for kt in range(KT):
-            nc.scalar.copy(dx[kt][:, S - P : S], last_banks[kt][:, 0, :])
+        nc.scalar.copy(dx[0][:, S - P : S], last_banks[0][:, 0, :])
+        nc.vector.tensor_copy(dx[1][:, S - P : S], last_banks[1][:, 0, :])
 
         first = [keep.tile([P, T], F32, name="first_%d" % kt, tag="apart_%d" % kt, align_bytes=64) for kt in range(KT)]
         total = [keep.tile([P, T], F32, name="total_%d" % kt, tag="y_%d" % kt, align_bytes=64) for kt in range(KT)]
-        for kt in range(KT):
-            nc.vector.tensor_copy(first[kt][:], dx[kt][:].indirect(pos1_sb[:]))
-        for kt, t0, t1, queue in ((0, 0, T, nc.sync), (1, 0, 512, nc.sync), (1, 512, T, nc.scalar)):
-            nc.vector.tensor_tensor(
-                total[kt][:, t0:t1], dx[kt][:].indirect(pos2_sb[:, t0 // 16 : t1 // 16]), first[kt][:, t0:t1], ALU.add
-            )
-            queue.dma_start(out=out[kt * P : (kt + 1) * P, t0:t1], in_=total[kt][:, t0:t1])
+
+        def offsets(tile, t0, t1):
+            return tile[:, t0 // 16 : t1 // 16]
+
+        def add_second(kt, t0, t1):
+            nc.vector.tensor_tensor(total[kt][:, t0:t1], dx[kt][:].indirect(offsets(pos2_sb, t0, t1)), first[kt][:, t0:t1], ALU.add)
+
+        def store(kt, t0, t1):
+            nc.sync.dma_start(out=out[kt * P : (kt + 1) * P, t0:t1], in_=total[kt][:, t0:t1])
+
+        nc.vector.tensor_copy(first[1][:, 0:VECTOR_FIRST], dx[1][:].indirect(offsets(pos1_sb, 0, VECTOR_FIRST)))
+        for kt, t0, t1 in ((0, 0, C), (0, C, T), (1, VECTOR_FIRST, T)):
+            nc.scalar.activation(first[kt][:, t0:t1], dx[kt][:].indirect(offsets(pos1_sb, t0, t1)), ACT.Copy)
+        add_second(0, 0, C)
+        add_second(1, 0, VECTOR_FIRST)
+        add_second(0, C, T)
+        store(0, 0, T)
+        add_second(1, VECTOR_FIRST, 2 * C)
+        store(1, 0, 2 * C)
+        add_second(1, 2 * C, T)
+        store(1, 2 * C, T)

@@ -118,7 +118,10 @@ def tile_moe_bdx_glu_silu_kernel(
         def gather_bytes(j0, j1):
             nc.vector.tensor_copy(g_s[:, j0:j1], dy_s[:].indirect(offs_sb[:, j0 // 16 : j1 // 16]))
 
-        y_sb, da_sb, codes, scales, th, rest, apart, m_sb = {}, {}, {}, {}, {}, {}, {}, {}
+        y_sb, th, rest, apart, m_sb = {}, {}, {}, {}, {}
+        da_sb = keep.tile([P, 2 * E * G, P * PACK], BF16, name="da_sb", align_bytes=64)
+        codes = keep.tile([P, 2 * E * G, P], U32, name="codes", align_bytes=64)
+        scales = keep.tile([P, 2 * E * G, P], U8, name="scales", align_bytes=64)
         sig = keep.tile([P, E * G, PACK, P], F32, name="sig")
         dx = []
         last = E * G - 1
@@ -187,40 +190,34 @@ def tile_moe_bdx_glu_silu_kernel(
                 nc.tensor.transpose(turned(n)[:, t, :], m_sb[n][:, t, :], ident[:])
 
         def place(n, w):
-            return divmod(2 * n + 2 - w, 4)
+            return 2 * n + 1 - w
 
         def make_da(n, w):
-            j, k = place(n, w)
-            if j not in da_sb:
-                da_sb[j] = keep.tile([P, 4, P * PACK], BF16, name="da_%d" % j, tag="da_%d" % (j % 4), align_bytes=64)
             factor = by_group((y_sb, a1_sb)[w], n)
             nc.vector.tensor_tensor(
-                da_sb[j][:, k, :].rearrange("p (c i t) -> p c t i", i=RUN, t=PACK),
+                da_sb[:, place(n, w), :].rearrange("p (c i t) -> p c t i", i=RUN, t=PACK),
                 turned(n)[:].rearrange("p t (c i) -> p c t i", i=RUN),
                 factor.rearrange("p t (c i) -> p c t i", i=RUN),
                 ALU.mult,
             )
 
-        def quantize(j, k0, k1):
-            if j not in codes:
-                codes[j] = keep.tile([P, 4, P], U32, name="codes_%d" % j, align_bytes=64)
-                scales[j] = keep.tile([P, 4, P], U8, name="scales_%d" % j, align_bytes=64)
+        def quantize(k0, k1):
             nc.vector.quantize_mx(
-                out=codes[j][:, k0:k1, :].rearrange("p k j -> p (k j)").bitcast(FP8X4),
-                scales=scales[j][:, k0:k1, :].rearrange("p k j -> p (k j)"),
-                in_=da_sb[j][:, k0:k1, :].rearrange("p k j -> p (k j)"),
+                out=codes[:, k0:k1, :].rearrange("p k j -> p (k j)").bitcast(FP8X4),
+                scales=scales[:, k0:k1, :].rearrange("p k j -> p (k j)"),
+                in_=da_sb[:, k0:k1, :].rearrange("p k j -> p (k j)"),
             )
 
         def second_pass(out_cols, n, kt, w, start, stop):
             e = n // G
-            j, k = place(n, w)
+            k = place(n, w)
             words, plane = ((w1_w, w1_s), (w3_w, w3_s))[w]
             nc.tensor.matmul_mx(
                 out=out_cols,
                 lhsT=words[:, e, 2 * kt * P : 2 * (kt + 1) * P].bitcast(FP4X4),
                 lhsT_scale=plane[:, e, kt * P : (kt + 1) * P],
-                rhs=codes[j][:, k, :].bitcast(FP8X4),
-                rhs_scale=scales[j][:, k, :],
+                rhs=codes[:, k, :].bitcast(FP8X4),
+                rhs_scale=scales[:, k, :],
                 start=start, stop=stop,
             )
 
@@ -276,33 +273,32 @@ def tile_moe_bdx_glu_silu_kernel(
                         rest_apart(k)
                         nc.gpsimd.tensor_tensor(by_group(y_sb, k), apart[k][:], by_group(a3_sb, k), ALU.mult)
             if e == E - 2:
-                for b, (n0, n1) in enumerate(((0, 1), (1, 3), (3, 5))):
+                for b, (n0, n1) in enumerate(((0, 1), (1, 3))):
                     second_product(n0, n1, side_banks[b])
             make_da(n, 1)
+            if e in (2, 4):
+                quantize(4 * (e - 2), 4 * e)
+            if e == E - 2:
+                second_product(3, 5, side_banks[2])
+                second_product(5, 7, side_banks[3])
             make_da(n + 1, 1)
             first_product(n + 2)
             make_da(n, 0)
             first_product(n + 3)
             make_da(n + 1, 0)
-            if e == 0:
-                quantize(0, 1, 2)
-                quantize(0, 2, 4)
-            else:
-                quantize(e, 0, 4)
-        second_product(5, 7, side_banks[3])
+        quantize(place(last - 3, 1), place(last - 2, 0))
         second_product(7, 9, group_banks[2])
         make_da(last - 1, 1)
         make_da(last - 1, 0)
-        quantize(E - 1, 0, 2)
+        quantize(place(last - 2, 0), place(last - 1, 0))
         second_product(9, 10, group_banks[3])
         make_da(last, 1)
-        quantize(E - 1, 2, 3)
+        quantize(place(last - 1, 0), place(last, 1))
         second_product(10, 11, side_banks[2])
         make_da(last, 0)
         last_banks = group_banks[0:KT]
         for w in (1, 0):
-            j, k = place(last, w)
-            quantize(j, k, k + 1)
+            quantize(place(last, w), place(last, w) + 1)
             for kt in range(KT):
                 second_pass(last_banks[kt][:, 0, :], last, kt, w, w == 1, w == 0)
         nc.scalar.copy(dx[0][:, S - P : S], last_banks[0][:, 0, :])
@@ -321,13 +317,14 @@ def tile_moe_bdx_glu_silu_kernel(
             nc.sync.dma_start(out=out[kt * P : (kt + 1) * P, t0:t1], in_=total[kt][:, t0:t1])
 
         nc.vector.tensor_copy(first[1][:, 0:VECTOR_FIRST], dx[1][:].indirect(offsets(pos1_sb, 0, VECTOR_FIRST)))
-        for kt, t0, t1 in ((0, 0, C), (0, C, T), (1, VECTOR_FIRST, T)):
+        for kt, t0, t1 in ((0, 0, 128), (0, 128, 384), (0, 384, T), (1, VECTOR_FIRST, 480), (1, 480, T)):
             nc.scalar.activation(first[kt][:, t0:t1], dx[kt][:].indirect(offsets(pos1_sb, t0, t1)), ACT.Copy)
-        add_second(0, 0, C)
+        add_second(0, 0, 128)
         add_second(1, 0, VECTOR_FIRST)
-        add_second(0, C, T)
+        add_second(0, 128, 384)
+        add_second(0, 384, T)
         store(0, 0, T)
-        add_second(1, VECTOR_FIRST, 2 * C)
-        store(1, 0, 2 * C)
-        add_second(1, 2 * C, T)
-        store(1, 2 * C, T)
+        add_second(1, VECTOR_FIRST, 480)
+        store(1, 0, 480)
+        add_second(1, 480, T)
+        store(1, 480, T)

@@ -13,6 +13,7 @@ GROUP_BANKS = 4
 RUN = 2
 OFF_VECTOR = (2, 3)
 VECTOR_FIRST = 192
+SCALAR_BOTH = 576
 
 FLOPS = 2 * S * (N * H + 2 * H * K)
 BYTES = 4 * (2 * H * S + S + K * T) + (N * T + N * T // 32) + E * (N * H + 2 * H * K) * 17 // 32 + 2 * P * (S + 2 * T) // 16
@@ -88,12 +89,13 @@ def tile_moe_bdx_glu_silu_kernel(
         nc.sync.dma_start(offs_sb[:], offs)
         for r in range(4):
             nc.sync.dma_start(out=dy_s[r:P:32, :].bitcast(I32), in_=dy_scales[0, r:16:4, :].bitcast(I32))
-        load_saved(a1_sb, a1, "a1", 0, 1, nc.scalar)
-        nc.sync.dma_start(out=dy_w[:], in_=dy_words[0].rearrange("p t d -> p (t d)").bitcast(I32))
+        a1_first = [keep.tile([P, PACK, P], F32, name="a1_first_%d" % g) for g in range(G)]
+        for g, queue in enumerate((nc.scalar, nc.sync)):
+            queue.dma_start(out=a1_first[g][:], in_=a1[:, g * P : (g + 1) * P].rearrange("(p t) c -> p t c", t=PACK))
         load_saved(a1_sb, a1, "a1", 1, 2)
+        nc.sync.dma_start(out=dy_w[:], in_=dy_words[0].rearrange("p t d -> p (t d)").bitcast(I32))
         nc.sync.dma_start(out=gate_rows[0:PACK, :], in_=gate[0, :].rearrange("(r c) -> r c", r=PACK))
         nc.sync.dma_start(pos1_sb[:], pos1)
-        nc.sync.dma_start(pos2_sb[:], pos2)
         load_words(w2_w, w2_words, 0, 2)
         load_saved(a3_sb, a3, "a3", 0, 1)
         load_scales(w2_s, w2_scales)
@@ -111,6 +113,7 @@ def tile_moe_bdx_glu_silu_kernel(
         load_scales(w3_s, w3_scales)
         load_words(w3_w, w3_words, 0, E)
         load_words(w1_w, w1_words, 0, E)
+        nc.sync.dma_start(pos2_sb[:], pos2)
 
         def gather_words(j0, j1):
             nc.vector.tensor_copy(g_w[:, j0 % (S - C) : j0 % (S - C) + j1 - j0], dy_w[:].bitcast(U32).indirect(offs_sb[:, j0 // 16 : j1 // 16]))
@@ -127,11 +130,17 @@ def tile_moe_bdx_glu_silu_kernel(
         last = E * G - 1
 
         def by_group(saved, n):
+            if n // G not in saved:
+                return a1_first[n][:]
             return saved[n // G][:, :, n % G * P : (n % G + 1) * P]
 
         def make_silu(e):
             rest[e] = keep.tile([P, PACK, C], F32, name="rest_%d" % e, tag={1: "rest_1", 2: "rest_2", E - 1: "dx_1"}.get(e, "chain_%d" % e), align_bytes=64)
-            nc.scalar.activation(rest[e][:], a1_sb[e], ACT.Silu, scale=-1.0)
+            if e > 0:
+                nc.scalar.activation(rest[e][:], a1_sb[e], ACT.Silu, scale=-1.0)
+                return
+            for g in range(G):
+                nc.scalar.activation(by_group(rest, g), a1_first[g][:], ACT.Silu, scale=-1.0)
 
         def make_rest(e):
             nc.scalar.activation(rest[e][:], rest[e][:], ACT.Identity, bias=1.0, scale=-1.0)
@@ -233,6 +242,13 @@ def tile_moe_bdx_glu_silu_kernel(
                     dx[kt][:, n0 * P : n1 * P].rearrange("p (g j) -> p g j", j=P), bank[:, kt * G : kt * G + n1 - n0, :]
                 )
 
+        def second_product_wide(n0, n1, banks):
+            for kt in range(KT):
+                for n in range(n0, n1):
+                    for w in range(2):
+                        second_pass(banks[kt][:, n - n0, :], n, kt, w, w == 0, w == 1)
+                nc.scalar.copy(dx[kt][:, n0 * P : n1 * P].rearrange("p (g j) -> p g j", j=P), banks[kt][:, 0 : n1 - n0, :])
+
         for j0 in range(0, S, 2 * C):
             gather_bytes(j0, j0 + 2 * C)
         for j0, j1 in ((0, 2 * C), (2 * C, 4 * C), (4 * C, 5 * C)):
@@ -279,8 +295,7 @@ def tile_moe_bdx_glu_silu_kernel(
             if e in (2, 4):
                 quantize(4 * (e - 2), 4 * e)
             if e == E - 2:
-                second_product(3, 5, side_banks[2])
-                second_product(5, 7, side_banks[3])
+                second_product_wide(3, 7, side_banks[2:4])
             make_da(n + 1, 1)
             first_product(n + 2)
             make_da(n, 0)
@@ -291,10 +306,9 @@ def tile_moe_bdx_glu_silu_kernel(
         make_da(last - 1, 1)
         make_da(last - 1, 0)
         quantize(place(last - 2, 0), place(last - 1, 0))
-        second_product(9, 10, group_banks[3])
         make_da(last, 1)
         quantize(place(last - 1, 0), place(last, 1))
-        second_product(10, 11, side_banks[2])
+        second_product_wide(9, 11, side_banks[2:4])
         make_da(last, 0)
         last_banks = group_banks[0:KT]
         for w in (1, 0):
@@ -316,15 +330,19 @@ def tile_moe_bdx_glu_silu_kernel(
         def store(kt, t0, t1):
             nc.sync.dma_start(out=out[kt * P : (kt + 1) * P, t0:t1], in_=total[kt][:, t0:t1])
 
+        second = keep.tile([P, T - SCALAR_BOTH], F32, name="second", align_bytes=64)
         nc.vector.tensor_copy(first[1][:, 0:VECTOR_FIRST], dx[1][:].indirect(offsets(pos1_sb, 0, VECTOR_FIRST)))
-        for kt, t0, t1 in ((0, 0, 128), (0, 128, 384), (0, 384, T), (1, VECTOR_FIRST, 480), (1, 480, T)):
+        for kt, t0, t1 in ((0, 0, 128), (0, 128, 384), (0, 384, T), (1, VECTOR_FIRST, SCALAR_BOTH), (1, SCALAR_BOTH, T)):
             nc.scalar.activation(first[kt][:, t0:t1], dx[kt][:].indirect(offsets(pos1_sb, t0, t1)), ACT.Copy)
+        nc.scalar.activation(second[:], dx[1][:].indirect(offsets(pos2_sb, SCALAR_BOTH, T)), ACT.Copy)
         add_second(0, 0, 128)
         add_second(1, 0, VECTOR_FIRST)
+        store(1, 0, VECTOR_FIRST)
         add_second(0, 128, 384)
+        store(0, 0, 384)
         add_second(0, 384, T)
-        store(0, 0, T)
-        add_second(1, VECTOR_FIRST, 480)
-        store(1, 0, 480)
-        add_second(1, 480, T)
-        store(1, 480, T)
+        store(0, 384, T)
+        add_second(1, VECTOR_FIRST, SCALAR_BOTH)
+        store(1, VECTOR_FIRST, SCALAR_BOTH)
+        nc.vector.tensor_tensor(total[1][:, SCALAR_BOTH:T], first[1][:, SCALAR_BOTH:T], second[:], ALU.add)
+        store(1, SCALAR_BOTH, T)

@@ -11,7 +11,8 @@ G = C // P
 KT = K // P
 GROUP_BANKS = 4
 RUN = 2
-OFF_VECTOR = (2, 3)
+OFF_VECTOR = (3, 7)
+AFFINE_ON_GPSIMD = (7,)
 VECTOR_FIRST = 192
 SCALAR_BOTH = 576
 
@@ -121,7 +122,7 @@ def tile_moe_bdx_glu_silu_kernel(
         def gather_bytes(j0, j1):
             nc.vector.tensor_copy(g_s[:, j0:j1], dy_s[:].indirect(offs_sb[:, j0 // 16 : j1 // 16]))
 
-        y_sb, th, rest, apart, m_sb = {}, {}, {}, {}, {}
+        y_sb, th, rest, m_sb = {}, {}, {}, {}
         da_sb = keep.tile([P, 2 * E * G, P * PACK], BF16, name="da_sb", align_bytes=64)
         codes = keep.tile([P, 2 * E * G, P], U32, name="codes", align_bytes=64)
         scales = keep.tile([P, 2 * E * G, P], U8, name="scales", align_bytes=64)
@@ -135,7 +136,7 @@ def tile_moe_bdx_glu_silu_kernel(
             return saved[n // G][:, :, n % G * P : (n % G + 1) * P]
 
         def make_silu(e):
-            rest[e] = keep.tile([P, PACK, C], F32, name="rest_%d" % e, tag={1: "rest_1", 2: "rest_2", E - 1: "dx_1"}.get(e, "chain_%d" % e), align_bytes=64)
+            rest[e] = keep.tile([P, PACK, C], F32, name="rest_%d" % e, tag={1: "rest_1", 2: "rest_2", 3: "rest_1", E - 1: "dx_1"}.get(e, "chain_%d" % e), align_bytes=64)
             if e > 0:
                 nc.scalar.activation(rest[e][:], a1_sb[e], ACT.Silu, scale=-1.0)
                 return
@@ -144,10 +145,6 @@ def tile_moe_bdx_glu_silu_kernel(
 
         def make_rest(e):
             nc.scalar.activation(rest[e][:], rest[e][:], ACT.Identity, bias=1.0, scale=-1.0)
-
-        def rest_apart(n):
-            apart[n] = keep.tile([P, PACK, P], F32, name="rest_group_%d" % n, tag="th_%d" % (2 * (n % G) + 1), align_bytes=64)
-            nc.scalar.activation(apart[n][:], by_group(rest, n), ACT.Identity, bias=1.0, scale=-1.0)
 
         def rest_on_gpsimd(e, tag):
             neg = rest[e]
@@ -169,6 +166,10 @@ def tile_moe_bdx_glu_silu_kernel(
             nc.scalar.activation(th[n][:], a1_t[:], ACT.Tanh, scale=0.5)
 
         def make_sigmoid(n):
+            if n in AFFINE_ON_GPSIMD:
+                nc.gpsimd.tensor_scalar(sig[:, n, :, :], th[n][:], 0.5, 0.5, ALU.mult, ALU.add)
+                gate_off_vector(n)
+                return
             nc.scalar.activation(sig[:, n, :, :], th[n][:], ACT.Identity, bias=0.5, scale=0.5)
 
         def turned(n):
@@ -230,19 +231,9 @@ def tile_moe_bdx_glu_silu_kernel(
                 start=start, stop=stop,
             )
 
-        def second_product(n0, n1, bank):
+        def second_product_wide(n0, n1, banks):
             if not dx:
                 dx.extend(keep.tile([P, S], F32, name="dx_%d" % kt, tag="dx_%d" % kt, align_bytes=64) for kt in range(KT))
-            for kt in range(KT):
-                for n in range(n0, n1):
-                    for w in range(2):
-                        second_pass(bank[:, kt * G + n - n0, :], n, kt, w, w == 0, w == 1)
-            for kt in range(KT):
-                nc.scalar.copy(
-                    dx[kt][:, n0 * P : n1 * P].rearrange("p (g j) -> p g j", j=P), bank[:, kt * G : kt * G + n1 - n0, :]
-                )
-
-        def second_product_wide(n0, n1, banks):
             for kt in range(KT):
                 for n in range(n0, n1):
                     for w in range(2):
@@ -269,8 +260,7 @@ def tile_moe_bdx_glu_silu_kernel(
                 nc.scalar.copy(gate_col[:].rearrange("p (r b) -> p r b", b=blocks), group_banks[3][:, 0:blocks, 0:PACK].rearrange("p b r -> p r b"))
         first_product(0)
         first_product(1)
-        for n in OFF_VECTOR:
-            gate_off_vector(n)
+        gate_off_vector(OFF_VECTOR[0])
         make_y(1, "y_1", G)
         gather_words(S - C, S)
         for e in range(E - 1):
@@ -280,41 +270,39 @@ def tile_moe_bdx_glu_silu_kernel(
                     for g in range(G):
                         step(n + 4 + g)
                 make_silu(e + 2)
-                if e < 3:
+                if e < 2:
                     make_rest(e + 2)
-                    make_y(e + 2, "y_%d" % (e + 2), 1 if e < 2 else G)
                 else:
-                    y_sb[E - 1] = keep.tile([P, PACK, C], F32, name="y_last")
-                    for k in (last - 1, last):
-                        rest_apart(k)
-                        nc.gpsimd.tensor_tensor(by_group(y_sb, k), apart[k][:], by_group(a3_sb, k), ALU.mult)
+                    rest_on_gpsimd(e + 2, "apart_%d" % (e % 2))
+                make_y(e + 2, "y_%d" % (e + 2), 1 if e < 2 else G)
             if e == E - 2:
-                for b, (n0, n1) in enumerate(((0, 1), (1, 3))):
-                    second_product(n0, n1, side_banks[b])
+                second_product_wide(0, 2, side_banks[0:2])
             make_da(n, 1)
             if e in (2, 4):
                 quantize(4 * (e - 2), 4 * e)
             if e == E - 2:
-                second_product_wide(3, 7, side_banks[2:4])
+                second_product_wide(2, 6, side_banks[2:4])
             make_da(n + 1, 1)
             first_product(n + 2)
             make_da(n, 0)
             first_product(n + 3)
             make_da(n + 1, 0)
         quantize(place(last - 3, 1), place(last - 2, 0))
-        second_product(7, 9, group_banks[2])
+        second_product_wide(6, 9, group_banks[2:4])
         make_da(last - 1, 1)
-        make_da(last - 1, 0)
-        quantize(place(last - 2, 0), place(last - 1, 0))
         make_da(last, 1)
+        quantize(place(last - 2, 0), place(last - 1, 0))
+        make_da(last - 1, 0)
+        quantize(place(last, 1), place(last, 0))
         quantize(place(last - 1, 0), place(last, 1))
         second_product_wide(9, 11, side_banks[2:4])
-        make_da(last, 0)
         last_banks = group_banks[0:KT]
-        for w in (1, 0):
-            quantize(place(last, w), place(last, w) + 1)
-            for kt in range(KT):
-                second_pass(last_banks[kt][:, 0, :], last, kt, w, w == 1, w == 0)
+        for kt in range(KT):
+            second_pass(last_banks[kt][:, 0, :], last, kt, 1, True, False)
+        make_da(last, 0)
+        quantize(place(last, 0), place(last, 0) + 1)
+        for kt in range(KT):
+            second_pass(last_banks[kt][:, 0, :], last, kt, 0, False, True)
         nc.scalar.copy(dx[0][:, S - P : S], last_banks[0][:, 0, :])
         nc.vector.tensor_copy(dx[1][:, S - P : S], last_banks[1][:, 0, :])
 

from contextlib import ExitStack

import concourse.mybir as mybir
from concourse.masks import make_identity

K, T, E, C, H, N = 256, 768, 6, 256, 512, 512
S = E * C
P = 128
PACK = 4
G = C // P
KT = K // P
GROUP_BANKS = 4
RUN = 2
OFF_VECTOR = (3, 7)
AFFINE_ON_GPSIMD = (7,)
VECTOR_FIRST = 192
SCALAR_BOTH = 576

FLOPS = 2 * S * (N * H + 2 * H * K)
BYTES = 4 * (2 * H * S + S + K * T) + (N * T + N * T // 32) + E * (N * H + 2 * H * K) * 17 // 32 + 2 * P * (S + 2 * T) // 16

F32 = mybir.dt.float32
BF16 = mybir.dt.bfloat16
I32 = mybir.dt.int32
U32 = mybir.dt.uint32
U16 = mybir.dt.uint16
U8 = mybir.dt.uint8
FP8X4 = mybir.dt.float8_e4m3fn_x4
FP4X4 = mybir.dt.float4_e2m1fn_x4
ACT = mybir.ActivationFunctionType
ALU = mybir.AluOpType


def tile_moe_bdx_glu_silu_kernel(
    tc, dy_words, dy_scales, a1, a3, w2_words, w2_scales, w1_words, w1_scales,
    w3_words, w3_scales, gate, offs, pos1, pos2, out,
):
    nc = tc.nc
    with ExitStack() as ctx:
        keep = ctx.enter_context(tc.tile_pool(name="keep", bufs=1))
        ring = ctx.enter_context(tc.tile_pool(name="ring", bufs=3))
        psum = ctx.enter_context(tc.psum_pool(name="psum", bufs=1))
        group_banks = [psum.tile([P, PACK, P], F32, name="group_bank_%d" % b) for b in range(GROUP_BANKS)]
        side_banks = [psum.tile([P, PACK, P], F32, name="side_bank_%d" % b) for b in range(4)]

        offs_sb = keep.tile([P, S // 16], U16, name="offs_sb")
        pos1_sb = keep.tile([P, T // 16], U16, name="pos1_sb")
        pos2_sb = keep.tile([P, T // 16], U16, name="pos2_sb")
        dy_w = keep.tile([P, T], I32, name="dy_w", align_bytes=64)
        dy_s = keep.tile([P, T], U8, name="dy_s", align_bytes=64)
        g_w = keep.tile([P, S - C], U32, name="g_w", align_bytes=64)
        g_s = keep.tile([P, S], U8, name="g_s", align_bytes=64)
        w2_w = keep.tile([P, E, 2 * H], U8, name="w2_w", align_bytes=64)
        w1_w = keep.tile([P, E, 2 * K], U8, name="w1_w", align_bytes=64)
        w3_w = keep.tile([P, E, 2 * K], U8, name="w3_w", align_bytes=64)
        w2_s = keep.tile([P, E, H], U8, name="w2_s", align_bytes=64)
        w1_s = keep.tile([P, E, K], U8, name="w1_s", align_bytes=64)
        w3_s = keep.tile([P, E, K], U8, name="w3_s", align_bytes=64)
        gate_rows = keep.tile([P, S // PACK], F32, name="gate_rows")
        gate_col = keep.tile([P, E * G], F32, name="gate_col")
        ident = keep.tile([P, P], F32, name="ident")
        a1_sb, a3_sb = {}, {}

        nc.gpsimd.memset(dy_s[:].bitcast(I32), 0)
        nc.gpsimd.memset(gate_rows[:], 0.0)
        make_identity(nc, ident[:])
        nc.gpsimd.memset(w2_s[:].bitcast(I32), 0)
        nc.gpsimd.memset(w1_s[:].bitcast(I32), 0)
        nc.gpsimd.memset(w3_s[:].bitcast(I32), 0)

        def load_scales(plane, src):
            for r in range(4):
                nc.sync.dma_start(
                    out=plane[r:P:32, :, :].bitcast(I32),
                    in_=src[:, 0, r:16:4, :].rearrange("e q i -> q e i").bitcast(I32),
                )

        def load_words(tile, src, e0, e1):
            nc.sync.dma_start(
                out=tile[:, e0:e1, :].bitcast(I32),
                in_=src[e0:e1, 0, :, :].rearrange("e p b -> p e b").bitcast(I32),
            )

        def load_saved(views, src, name, e0, e1, queue=nc.sync):
            tile = keep.tile([P, PACK, (e1 - e0) * C], F32, name="%s_%d" % (name, e0))
            queue.dma_start(out=tile[:], in_=src[:, e0 * C : e1 * C].rearrange("(p t) c -> p t c", t=PACK))
            for e in range(e0, e1):
                views[e] = tile[:, :, (e - e0) * C : (e - e0 + 1) * C]

        nc.sync.dma_start(offs_sb[:], offs)
        for r in range(4):
            nc.sync.dma_start(out=dy_s[r:P:32, :].bitcast(I32), in_=dy_scales[0, r:16:4, :].bitcast(I32))
        a1_first = [keep.tile([P, PACK, P], F32, name="a1_first_%d" % g) for g in range(G)]
        for g, queue in enumerate((nc.scalar, nc.sync)):
            queue.dma_start(out=a1_first[g][:], in_=a1[:, g * P : (g + 1) * P].rearrange("(p t) c -> p t c", t=PACK))
        load_saved(a1_sb, a1, "a1", 1, 2)
        nc.sync.dma_start(out=dy_w[:], in_=dy_words[0].rearrange("p t d -> p (t d)").bitcast(I32))
        nc.sync.dma_start(out=gate_rows[0:PACK, :], in_=gate[0, :].rearrange("(r c) -> r c", r=PACK))
        nc.sync.dma_start(pos1_sb[:], pos1)
        load_words(w2_w, w2_words, 0, 2)
        load_saved(a3_sb, a3, "a3", 0, 1)
        load_scales(w2_s, w2_scales)
        load_saved(a1_sb, a1, "a1", 2, 3)
        load_saved(a3_sb, a3, "a3", 1, 2)
        load_saved(a1_sb, a1, "a1", 3, 4)
        load_words(w2_w, w2_words, 2, 4)
        load_saved(a1_sb, a1, "a1", 4, 5)
        load_saved(a3_sb, a3, "a3", 2, 3)
        load_words(w2_w, w2_words, 4, E)
        load_saved(a1_sb, a1, "a1", 5, 6)
        for e in range(3, E):
            load_saved(a3_sb, a3, "a3", e, e + 1)
        load_scales(w1_s, w1_scales)
        load_scales(w3_s, w3_scales)
        load_words(w3_w, w3_words, 0, E)
        load_words(w1_w, w1_words, 0, E)
        nc.sync.dma_start(pos2_sb[:], pos2)

        def gather_words(j0, j1):
            nc.vector.tensor_copy(g_w[:, j0 % (S - C) : j0 % (S - C) + j1 - j0], dy_w[:].bitcast(U32).indirect(offs_sb[:, j0 // 16 : j1 // 16]))

        def gather_bytes(j0, j1):
            nc.vector.tensor_copy(g_s[:, j0:j1], dy_s[:].indirect(offs_sb[:, j0 // 16 : j1 // 16]))

        y_sb, th, rest, m_sb = {}, {}, {}, {}
        da_sb = keep.tile([P, 2 * E * G, P * PACK], BF16, name="da_sb", align_bytes=64)
        codes = keep.tile([P, 2 * E * G, P], U32, name="codes", align_bytes=64)
        scales = keep.tile([P, 2 * E * G, P], U8, name="scales", align_bytes=64)
        sig = keep.tile([P, E * G, PACK, P], F32, name="sig")
        dx = []
        last = E * G - 1

        def by_group(saved, n):
            if n // G not in saved:
                return a1_first[n][:]
            return saved[n // G][:, :, n % G * P : (n % G + 1) * P]

        def make_silu(e):
            rest[e] = keep.tile([P, PACK, C], F32, name="rest_%d" % e, tag={1: "rest_1", 2: "rest_2", 3: "rest_1", E - 1: "dx_1"}.get(e, "chain_%d" % e), align_bytes=64)
            if e > 0:
                nc.scalar.activation(rest[e][:], a1_sb[e], ACT.Silu, scale=-1.0)
                return
            for g in range(G):
                nc.scalar.activation(by_group(rest, g), a1_first[g][:], ACT.Silu, scale=-1.0)

        def make_rest(e):
            nc.scalar.activation(rest[e][:], rest[e][:], ACT.Identity, bias=1.0, scale=-1.0)

        def rest_on_gpsimd(e, tag):
            neg = rest[e]
            rest[e] = keep.tile([P, PACK, C], F32, name="rest_apart_%d" % e, tag=tag, align_bytes=64)
            nc.gpsimd.tensor_scalar(rest[e][:], neg[:], -1.0, 1.0, ALU.mult, ALU.add)

        def make_y(e, tag, parts):
            y_sb[e] = keep.tile([P, PACK, C], F32, name="y_%d" % e, tag=tag, align_bytes=64)
            for j in range(0, C, C // parts):
                cols = slice(j, j + C // parts)
                nc.gpsimd.tensor_tensor(y_sb[e][:, :, cols], rest[e][:, :, cols], a3_sb[e][:, :, cols], ALU.mult)

        def make_tanh(n):
            tag = "dx_%d" % (1 - n % G) if n >= last - 1 else "chain_%d" % (n // G) if n % G == 0 and n > 0 else "th_%d" % n
            th[n] = keep.tile([P, PACK, P], F32, name="th_%d" % n, tag=tag, align_bytes=64)
            a1_t = side_banks[n % 4]
            for t in range(PACK):
                nc.tensor.transpose(a1_t[:, t, :], by_group(a1_sb, n)[:, t, :], ident[:])
            nc.scalar.activation(th[n][:], a1_t[:], ACT.Tanh, scale=0.5)

        def make_sigmoid(n):
            if n in AFFINE_ON_GPSIMD:
                nc.gpsimd.tensor_scalar(sig[:, n, :, :], th[n][:], 0.5, 0.5, ALU.mult, ALU.add)
                gate_off_vector(n)
                return
            nc.scalar.activation(sig[:, n, :, :], th[n][:], ACT.Identity, bias=0.5, scale=0.5)

        def turned(n):
            return group_banks[n % GROUP_BANKS] if n < last - 1 else side_banks[n % G]

        def first_sums(n, bank):
            e = n // G
            cols = slice(n * P % (S - C), n * P % (S - C) + P)
            acc = bank[:].rearrange("j t p -> j (t p)")
            nc.tensor.matmul_mx(
                out=acc, lhsT=g_w[:, cols].bitcast(FP8X4), lhsT_scale=g_s[:, n * P : (n + 1) * P],
                rhs=w2_w[:, e, :].bitcast(FP4X4), rhs_scale=w2_s[:, e, :], start=True, stop=True,
            )
            return acc.rearrange("j (p t) -> j t p", t=PACK)

        def gate_off_vector(n):
            sums = first_sums(n, side_banks[n % 4])
            m_sb[n] = keep.tile([P, PACK, P], F32, name="m_%d" % n)
            nc.scalar.activation(m_sb[n][:], sums, ACT.Copy, scale=gate_col[:, n : n + 1])
            nc.gpsimd.tensor_tensor(m_sb[n][:], m_sb[n][:], sig[:, n, :, :], ALU.mult)

        def first_product(n):
            if n not in OFF_VECTOR:
                sums = first_sums(n, group_banks[n % GROUP_BANKS])
                m_sb[n] = ring.tile([P, PACK, P], F32, name="m")
                nc.vector.scalar_tensor_tensor(m_sb[n][:], sums, gate_col[:, n : n + 1], sig[:, n, :, :], ALU.mult, ALU.mult)
            for t in range(PACK):
                nc.tensor.transpose(turned(n)[:, t, :], m_sb[n][:, t, :], ident[:])

        def place(n, w):
            return 2 * n + 1 - w

        def make_da(n, w):
            factor = by_group((y_sb, a1_sb)[w], n)
            nc.vector.tensor_tensor(
                da_sb[:, place(n, w), :].rearrange("p (c i t) -> p c t i", i=RUN, t=PACK),
                turned(n)[:].rearrange("p t (c i) -> p c t i", i=RUN),
                factor.rearrange("p t (c i) -> p c t i", i=RUN),
                ALU.mult,
            )

        def quantize(k0, k1):
            nc.vector.quantize_mx(
                out=codes[:, k0:k1, :].rearrange("p k j -> p (k j)").bitcast(FP8X4),
                scales=scales[:, k0:k1, :].rearrange("p k j -> p (k j)"),
                in_=da_sb[:, k0:k1, :].rearrange("p k j -> p (k j)"),
            )

        def second_pass(out_cols, n, kt, w, start, stop):
            e = n // G
            k = place(n, w)
            words, plane = ((w1_w, w1_s), (w3_w, w3_s))[w]
            nc.tensor.matmul_mx(
                out=out_cols,
                lhsT=words[:, e, 2 * kt * P : 2 * (kt + 1) * P].bitcast(FP4X4),
                lhsT_scale=plane[:, e, kt * P : (kt + 1) * P],
                rhs=codes[:, k, :].bitcast(FP8X4),
                rhs_scale=scales[:, k, :],
                start=start, stop=stop,
            )

        def second_product_wide(n0, n1, banks):
            if not dx:
                dx.extend(keep.tile([P, S], F32, name="dx_%d" % kt, tag="dx_%d" % kt, align_bytes=64) for kt in range(KT))
            for kt in range(KT):
                for n in range(n0, n1):
                    for w in range(2):
                        second_pass(banks[kt][:, n - n0, :], n, kt, w, w == 0, w == 1)
                nc.scalar.copy(dx[kt][:, n0 * P : n1 * P].rearrange("p (g j) -> p g j", j=P), banks[kt][:, 0 : n1 - n0, :])

        for j0 in range(0, S, 2 * C):
            gather_bytes(j0, j0 + 2 * C)
        for j0, j1 in ((0, 2 * C), (2 * C, 4 * C), (4 * C, 5 * C)):
            gather_words(j0, j1)
        make_silu(0)
        rest_on_gpsimd(0, "apart_0")
        make_y(0, "y_0", G)
        for e in range(2):
            for step in (make_tanh, make_sigmoid):
                for g in range(G):
                    step(e * G + g)
            if e == 0:
                make_silu(1)
                rest_on_gpsimd(1, "apart_1")
                blocks = S // PACK // P
                for b in range(blocks):
                    nc.tensor.transpose(group_banks[3][:, b, :], gate_rows[:, b * P : (b + 1) * P], ident[:])
                nc.scalar.copy(gate_col[:].rearrange("p (r b) -> p r b", b=blocks), group_banks[3][:, 0:blocks, 0:PACK].rearrange("p b r -> p r b"))
        first_product(0)
        first_product(1)
        gate_off_vector(OFF_VECTOR[0])
        make_y(1, "y_1", G)
        gather_words(S - C, S)
        for e in range(E - 1):
            n = e * G
            if e + 2 < E:
                for step in (make_tanh, make_sigmoid):
                    for g in range(G):
                        step(n + 4 + g)
                make_silu(e + 2)
                if e < 2:
                    make_rest(e + 2)
                else:
                    rest_on_gpsimd(e + 2, "apart_%d" % (e % 2))
                make_y(e + 2, "y_%d" % (e + 2), 1 if e < 2 else G)
            if e == E - 2:
                second_product_wide(0, 2, side_banks[0:2])
            make_da(n, 1)
            if e in (2, 4):
                quantize(4 * (e - 2), 4 * e)
            if e == E - 2:
                second_product_wide(2, 6, side_banks[2:4])
            make_da(n + 1, 1)
            first_product(n + 2)
            make_da(n, 0)
            first_product(n + 3)
            make_da(n + 1, 0)
        quantize(place(last - 3, 1), place(last - 2, 0))
        second_product_wide(6, 9, group_banks[2:4])
        make_da(last - 1, 1)
        make_da(last, 1)
        quantize(place(last - 2, 0), place(last - 1, 0))
        make_da(last - 1, 0)
        quantize(place(last, 1), place(last, 0))
        quantize(place(last - 1, 0), place(last, 1))
        second_product_wide(9, 11, side_banks[2:4])
        last_banks = group_banks[0:KT]
        for kt in range(KT):
            second_pass(last_banks[kt][:, 0, :], last, kt, 1, True, False)
        make_da(last, 0)
        quantize(place(last, 0), place(last, 0) + 1)
        for kt in range(KT):
            second_pass(last_banks[kt][:, 0, :], last, kt, 0, False, True)
        nc.scalar.copy(dx[0][:, S - P : S], last_banks[0][:, 0, :])
        nc.vector.tensor_copy(dx[1][:, S - P : S], last_banks[1][:, 0, :])

        first = [keep.tile([P, T], F32, name="first_%d" % kt, tag="apart_%d" % kt, align_bytes=64) for kt in range(KT)]
        total = [keep.tile([P, T], F32, name="total_%d" % kt, tag="y_%d" % kt, align_bytes=64) for kt in range(KT)]

        def offsets(tile, t0, t1):
            return tile[:, t0 // 16 : t1 // 16]

        def add_second(kt, t0, t1):
            nc.vector.tensor_tensor(total[kt][:, t0:t1], dx[kt][:].indirect(offsets(pos2_sb, t0, t1)), first[kt][:, t0:t1], ALU.add)

        def store(kt, t0, t1):
            nc.sync.dma_start(out=out[kt * P : (kt + 1) * P, t0:t1], in_=total[kt][:, t0:t1])

        second = keep.tile([P, T - SCALAR_BOTH], F32, name="second", align_bytes=64)
        nc.vector.tensor_copy(first[1][:, 0:VECTOR_FIRST], dx[1][:].indirect(offsets(pos1_sb, 0, VECTOR_FIRST)))
        for kt, t0, t1 in ((0, 0, 128), (0, 128, 384), (0, 384, T), (1, VECTOR_FIRST, SCALAR_BOTH), (1, SCALAR_BOTH, T)):
            nc.scalar.activation(first[kt][:, t0:t1], dx[kt][:].indirect(offsets(pos1_sb, t0, t1)), ACT.Copy)
        nc.scalar.activation(second[:], dx[1][:].indirect(offsets(pos2_sb, SCALAR_BOTH, T)), ACT.Copy)
        add_second(0, 0, 128)
        add_second(1, 0, VECTOR_FIRST)
        store(1, 0, VECTOR_FIRST)
        add_second(0, 128, 384)
        store(0, 0, 384)
        add_second(0, 384, T)
        store(0, 384, T)
        add_second(1, VECTOR_FIRST, SCALAR_BOTH)
        store(1, VECTOR_FIRST, SCALAR_BOTH)
        nc.vector.tensor_tensor(total[1][:, SCALAR_BOTH:T], first[1][:, SCALAR_BOTH:T], second[:], ALU.add)
        store(1, SCALAR_BOTH, T)
